import numpy as np, ml_dtypes
CORES = [36,164,52,180,100,228,116,244]
N = 8
import mx_ref
BF = ml_dtypes.bfloat16
def gcols(t, e):
    v = np.concatenate([t.reshape(8, 16, -1, 4), np.zeros((8, 16, 1, 4), BF)], axis=2)
    return np.ascontiguousarray(np.stack([v[g][:, e[g]] for g in range(8)])).reshape(128, -1)
def tile(rs):
    return np.stack(rs, axis=2).reshape(128, -1).astype(BF)
def cut(t, i, w=512):
    return t[:, w * i:w * i + w]
def pick(q, e):
    c = np.concatenate([q[0].reshape(128, -1, 4), np.zeros((128, 1, 4), np.uint8)], axis=1); s = np.concatenate([q[1], np.ones((16, 1), np.uint8)], axis=1)
    return (np.ascontiguousarray(c[:, e].reshape(128, -1)), np.ascontiguousarray(s[:, e]))
def join(*qs):
    return (np.concatenate([q[0] for q in qs], axis=1), np.concatenate([q[1] for q in qs], axis=1))
def put(q, e, v):
    c, s = q[0].reshape(128, -1, 4).copy(), q[1].copy(); c[:, e] = v[0].reshape(128, -1, 4); s[:, e] = v[1]
    return (c.reshape(128, -1), s)
def pk(c, s):
    return (np.ascontiguousarray(c), mx_ref.live(s))
def emit(q):
    return q[0], q[1]
def packed(v, rng):
    q = [mx_ref.quantize(np.ascontiguousarray(v[r])) for r in range(N)]
    return np.stack([a for a, b in q]), np.stack([mx_ref.plane(b, rng) for a, b in q])
def values_of_codes():
    e, c = np.zeros((128, 128, 4), np.float32), np.zeros((128, 2, 4), np.uint8)
    e[np.arange(128), np.arange(128), 0] = 1
    c[:127, :, 0] = np.arange(256).reshape(2, 128).T[:127]
    return mx_ref.matmul(mx_ref.quantize(e.reshape(128, 512).astype(BF)), (c.reshape(128, 8), np.full((16, 2), 127, np.uint8))).T.reshape(-1).astype(np.float64)
CODE_VALUE, SCALE_VALUE = values_of_codes(), 2.0 ** (np.arange(256) - 127.0)
def decode(q):
    return (CODE_VALUE[q[0]].reshape(16, 8, -1, 4) * SCALE_VALUE[q[1]][:, None, :, None] + 0.0).reshape(128, -1).astype(np.float32)
def f(rng, *shape):
    return mx_ref.flush((rng.standard_normal(shape, dtype=np.float32) * np.exp2(rng.integers(-2, 3, shape[:-1] + (1,)))).astype(BF))
def wide(rng, *shape, cols=0):
    v = rng.standard_normal(shape, dtype=np.float32) * np.exp2(rng.integers(-12, 13, shape)).astype(np.float32)
    if cols: v *= np.repeat(np.exp2(rng.integers(-cols, cols + 1, shape[:-2] + (1, shape[-1] // 4))) * (rng.random(shape[:-2] + (1, shape[-1] // 4)) > 0.0625), 4, axis=-1).astype(np.float32)
    return mx_ref.flush(v.astype(BF))
C, L, CAP, R = 480, 5, 160, 2
def windows(p):
    s = np.concatenate([p + np.float32(0.0), np.full((8, L - 1), np.inf, np.float32)], axis=1)
    return np.arange(C) + np.argmin(np.stack([s[:, i:i + C] for i in range(L)]), axis=0)
def coarse(v):
    v = np.array(v.astype(np.float32))
    v[np.abs(v) < np.float32(2.0 ** -16)] = 0
    return v.astype(BF)
def numbers_of(rng):
    return {"x": coarse(f(rng, N, 128, 4 * C)), "u": np.array(f(rng, N, 128, 512)), "v": np.array(f(rng, N, 128, 512))}
def sealed(rng, w):
    c, p = packed(np.ascontiguousarray(w).reshape(N, 128, 2048), rng)
    return {"wc": c, "ws": p}
def weights(rng, still=None):
    w = coarse(f(rng, N, 128, 2048)).reshape(N, 128, 4, 128, 4)
    if still is not None: w[:, :, :, np.flatnonzero(still)] = 0
    return sealed(rng, w)
def signs(rng):
    return np.stack([rng.permutation(8) % 2 * 2.0 - 1.0 for r in range(N)])
def plant(rng, s, z=np.ones(N)):
    d = numbers_of(rng)
    x = d["x"].astype(np.float32).reshape(N, 8, 16, C, 4)
    u = d["u"].reshape(N, 128, 128, 4)
    z = z.astype(np.float32).astype(BF)
    x[:, :, 0] = 0
    x[:, :, 0, :, 0] = signs(rng)[:, :, None]
    k = 8 + 2 * R
    x[:, :, k:] = rng.integers(4, 8, (N, 8, 16 - k, C, 4)) * rng.choice([-1.0, 1.0], (N, 8, 16 - k, C, 4)) * 2.0 ** -20
    for t in range(R):
        g = ((s[:, :, t, :, None] >> np.arange(8)) & 1) * np.exp2(np.arange(8) - 23.0)
        x[:, :, 8 + 2 * t] = g[..., :4]
        x[:, :, 9 + 2 * t] = g[..., 4:]
        u[:, :, t::16] = 0
        for h in range(0, 128, 16):
            u[:, h, h + t, 0] = z
            u[:, h + 8 + 2 * t:h + 10 + 2 * t, h + t] = z[:, None, None]
    i = np.arange(128) % 16
    return {"x": x.reshape(N, 128, 4 * C).astype(BF), "u": u.reshape(N, 128, 512), "v": d["v"], **weights(rng, (i == 0) | (i >= 8))}
def setup_inputs(rng):
    return {**numbers_of(rng), **weights(rng)}
def setup_inputs_ties(rng):
    d = numbers_of(rng)
    e = rng.permutation(N)
    x = d["x"].reshape(N, 8, 16, C, 4)
    for r in range(N):
        k = np.zeros(C, int) if r == e[0] else np.full(C, 2) if r == e[1] else rng.permutation(C) % 3
        a = x[r][:, :8, :3].copy()
        a[:, :, 2] = 0
        x[r][:, :8] = a[:, :, k]
    u = d["u"].reshape(N, 8, 16, 128, 4)
    for t in range(R): u[:, :, 8:, t::16] = 0
    return {"x": x.reshape(N, 128, 4 * C), "u": u.reshape(N, 128, 512), "v": d["v"], **weights(rng, np.arange(128) % 16 < 8)}
def setup_inputs_near(rng):
    j = np.arange(C)
    saw = 255 - (j + rng.integers(0, 12, (N, 8, R, 1))) % rng.integers(4, 13, (N, 8, R, 1))
    any8 = rng.integers(8, 16, (N, 8, R, C))
    b = np.stack([np.stack([rng.permutation(8) % 2 for t in range(R)], axis=1) for r in range(N)])
    return plant(rng, np.where(b[..., None] == 1, saw, any8), np.where(rng.permutation(N) < N // 2, 2.0 ** -30, 1.0))
def setup_inputs_slots(rng):
    j = np.arange(C)
    q = np.arange(C + 1)
    n = q + (C - 1 - q) // L + 1
    s = np.zeros((N, 8, R, C), int)
    for r in range(N):
        for t in range(R):
            want = rng.permutation(np.concatenate([[CAP - 1, CAP, CAP + 1, n[0], C], rng.integers(n[0], C + 1, 3)]))
            s[r, :, t] = np.where(j < np.searchsorted(n, want)[:, None], 0, 1 + (C - 1 - j) % L)
    return plant(rng, s)
def setup_inputs_huge(rng):
    d = numbers_of(rng)
    i = np.flatnonzero(np.arange(128) % 16 >= 14)
    x = 2.0 ** 30 * (0.7 + 0.3 * rng.random((N, 128, C, 4)))
    x[:, i] *= 0.25
    c = np.stack([rng.permutation(C) % 2 * 2.0 - 1.0 for r in range(N)])
    c[rng.permutation(N) < N // 2] = 1
    x *= c[:, None, :, None]
    u = d["u"].reshape(N, 128, 8, 16, 4)
    g = np.stack([signs(rng) for t in range(R)], axis=-1)
    a = 2.0 ** 30 * (0.7 + 0.3 * rng.random((N, 128, 8, R, 4))) * g[:, None, :, :, None]
    u[:, :, :, :R] = a.astype(np.float32).astype(BF)
    w = np.zeros((N, 128, 4, 128, 4), np.float32)
    for b in range(4): w[:, i, b, i, b] = 32
    return {"x": x.astype(np.float32).reshape(N, 128, 4 * C).astype(BF), "u": u.reshape(N, 128, 512), "v": d["v"], **sealed(rng, w.astype(BF))}
def setup_inputs_spread(rng):
    d = setup_inputs(rng)
    d["x"] = coarse(wide(rng, N, 128, 4 * C, cols=6))
    return d
def check_inputs(d):
    b = []
    for k in ("x", "u", "v"):
        a = np.abs(d[k].astype(np.float32))
        if not (np.isfinite(a).all() and ((a == 0) | (a >= 2.0 ** -30) & (a <= 2.0 ** 30)).all()): b.append("a value of " + k)
    return b
def reference(x, u, v, wc, ws):
    qu = [mx_ref.quantize(u[r]) for r in range(N)]
    lay = [pk(wc[r], ws[r]) for r in range(N)]
    now = [x[r] for r in range(N)]
    ol = np.zeros((N, 8, 2 * C), np.float32)
    for t in range(R):
        q = [mx_ref.quantize(now[r]) for r in range(N)]
        held = decode(join(*q))
        numbers, far = [], []
        for r in range(N):
            m = windows(mx_ref.matmul(qu[r], q[r])[t::16])
            hit = np.zeros((8, C), bool)
            np.put_along_axis(hit, m, True, axis=1)
            upto = np.add.accumulate(hit, axis=1, dtype=np.int64)
            n = np.take_along_axis(upto, m, axis=1) - 1
            first = np.argsort(~hit, axis=1, kind="stable")[:, :CAP]
            e = np.where(np.arange(CAP) < upto[:, -1:], first, -1)
            p = mx_ref.quantize(gcols(cut(held, r, 4 * C).astype(BF), e))
            w = lay[(r + 1 + t) % N]
            far.append(mx_ref.quantize(tile([mx_ref.matmul(pick(w, np.arange(128 * b, 128 * b + 128)), p) * np.float32(0.03125) for b in range(4)])))
            numbers.append(n)
            ol[r] = np.concatenate([m, n], axis=1)
        came = decode(join(*far)).astype(BF)
        for r in range(N):
            add = gcols(cut(came, r, 4 * CAP), np.where(numbers[r] < CAP, numbers[r], -1))
            now[r] = np.ascontiguousarray((cut(held, r, 4 * C) + add.astype(np.float32)).astype(BF))
    y = np.zeros((N, 128, C), np.float32)
    oc, osc = np.zeros((N, 128, 4 * C), np.uint8), np.zeros((N, 16, C), np.uint8)
    for r in range(N):
        last = mx_ref.quantize(now[r])
        y[r] = mx_ref.matmul(mx_ref.quantize(v[r]), last)
        oc[r], osc[r] = emit(last)
    return {"y": y, "ol": ol, "oc": oc, "osc": osc}

@@ -1,0 +1,440 @@
+from concourse.mybir import dt, AluOpType as A, AxisListType, ActivationFunctionType as AF
+
+C, CAP, NR = 480, 160, 2
+BLK = C // 16
+FW, DW = 496, 176
+TAW, ODD = 1376, 704
+EWID = 1472
+BIG = 9e29
+
+F32, BF, I32, U16, X4, U8 = "float32", "bfloat16", "int32", "uint16", "float8_e4m3fn_x4", "uint8"
+SCRATCH = {}
+
+
+def _sb(name, n, d):
+    SCRATCH[name] = ("sbuf", [128, n], d)
+
+
+for _n, _w in (("wl", 512), ("wr0", 512), ("wr1", 512), ("qu", 128), ("qv", 128), ("qe", 512), ("qx", C), ("qa", 512),
+               ("qb", 512), ("qy", C), ("qz", C), ("qp0", CAP), ("qp1", CAP), ("qh0", CAP), ("qh1", CAP)):
+    _sb(_n + "c", _w, X4)
+    _sb(_n + "s", _w, U8)
+_sb("hand", 256, X4)
+for _n, _w in (("xt", 4 * C), ("ut", 512), ("vt", 512), ("zi", 520), ("et", 1056), ("t1", 2048), ("t2", 4 * C),
+               ("fs", 4 * FW), ("dh", 4 * DW), ("gg", 2 * C), ("pt0", 4 * CAP), ("pt1", 4 * CAP), ("ht0", 4 * CAP),
+               ("ht1", 4 * CAP), ("ge", 192), ("rl", 192), ("sg", 160), ("pat", 160), ("m2", 160)):
+    _sb(_n, _w, BF)
+for _n, _w in (("kr", 48), ("j16", 32), ("vals", C), ("cf", 32), ("bl", 32), ("msk", 96), ("kt", 32), ("d0", 40),
+               ("caps", 48), ("er0", EWID), ("er1", EWID), ("ta", TAW), ("bb", 48),
+               ("dd", 40), ("hit", 32), ("u2", 32), ("hk", 32), ("xx", 32), ("apr", 32), ("yy", 32), ("bs", 8),
+               ("tb", 320), ("nw", 32), ("un", 32), ("x2", 32), ("y2", 32), ("mf", 32), ("nf", 32),
+               ("up", 128), ("ysb", C)):
+    _sb(_n, _w, F32)
+_sb("pi", 8, I32)
+_sb("ci", 8, I32)
+_sb("ai", 32, I32)
+for _n, _w in (("fore", 32), ("back", 32), ("boff", 8), ("ew", 2), ("pos", 32), ("eoff", 16), ("noff", 32)):
+    _sb(_n, _w, U16)
+for _b in range(8):
+    SCRATCH["ps%d" % _b] = ("psum", [128, 512], F32)
+
+NCS, NDS = 100, 24
+SEMAPHORES = ["w0", "w1", "hin", "sent"] + ["c%d" % _k for _k in range(NCS)] + ["d%d" % _k for _k in range(NDS)]
+
+
+def plan(g, T, ops):
+    queues = {"g": g, "v": g.vector, "s": g.scalar, "p": g.tensor, "y": g.sync}
+    node_of, members = [], {}
+    for k, o in enumerate(ops):
+        key = o["grp"] if o["grp"] is not None else k
+        node_of.append(key)
+        members.setdefault(key, []).append(k)
+    know = {q: 0 for q in queues}
+    at_issue, waits, touched = [], [], {}
+    for k, o in enumerate(ops):
+        deps = set(o["after"])
+        for acc, writes in [(a, False) for a in o["r"]] + [(a, True) for a in o["w"]]:
+            for j, cols, wrote in touched.get(acc[1], []):
+                bank = acc[1].startswith("ps") and ops[j]["q"] != o["q"]
+                if bank or ((writes or wrote) and cols & acc[2]):
+                    deps.add(j)
+        for acc in o["r"]:
+            touched.setdefault(acc[1], []).append((k, acc[2], False))
+        for acc in o["w"]:
+            touched.setdefault(acc[1], []).append((k, acc[2], True))
+        deps.discard(k)
+        q = o["q"]
+        if q is None:
+            at_issue.append(0)
+            waits.append([])
+            continue
+        need = {}
+        for j in deps:
+            if not know[q] >> j & 1:
+                nd = node_of[j]
+                assert nd != node_of[k] and max(members[nd]) < k, (o["name"], ops[j]["name"])
+                cl = 0
+                for m in members[nd]:
+                    cl |= at_issue[m] | 1 << m
+                need[nd] = cl
+        keep = [nd for nd in need
+                if not any(n2 != nd and all(need[n2] >> m & 1 for m in members[nd]) for n2 in need)]
+        keep.sort(key=lambda nd: max(members[nd]))
+        for nd in keep:
+            know[q] |= need[nd]
+        at_issue.append(know[q])
+        waits.append(keep)
+    waited = set(nd for w in waits for nd in w)
+    pools = {False: [["c%d" % k, 0, 0] for k in range(NCS)], True: [["d%d" % k, 0, 0] for k in range(NDS)]}
+    signal = {}
+    for k, o in enumerate(ops):
+        nd = node_of[k]
+        if nd in signal or nd not in waited:
+            continue
+        if o["q"] is None:
+            signal[nd] = o["sem"]
+            continue
+        pool = pools[o["dma"]]
+        for s in pool:
+            if all(s[2] & ~at_issue[m] == 0 for m in members[nd]):
+                break
+        else:
+            assert False, "out of semaphores"
+        pool.remove(s)
+        pool.append(s)
+        s[1] += (16 if o["dma"] else 1) * len(members[nd])
+        for m in members[nd]:
+            s[2] |= 1 << m
+        signal[nd] = (s[0], s[1])
+    for k, o in enumerate(ops):
+        if o["q"] is None:
+            continue
+        e = queues[o["q"]]
+        for nd in waits[k]:
+            e.wait_ge(T.sem[signal[nd][0]], signal[nd][1])
+        if o["fn"] is None:
+            continue
+        ins = o["fn"](e)
+        if node_of[k] in signal:
+            ins.then_inc(T.sem[signal[node_of[k]][0]], 16 if o["dma"] else 1)
+        else:
+            assert not o["dma"], o["name"]
+
+
+def helper_of(core, topo):
+    return [c for c in topo.cores_of(core) if topo.die(c) != topo.die(core)][0]
+
+
+def count(mask):
+    return bin(mask).count("1")
+
+
+def send(g, T, topo, src, dst, out, in_, sem, mask):
+    rid, pid = topo.addr(dst, src)
+    return g.remote_dma(out, in_, T.sem[sem], T.sem.sent, pid, rid, mask)
+
+
+def rank_program(g, core, T, topo):
+    cores = list(T.cores)
+    n = len(cores)
+    rank = T.rank_of(core)
+    if rank is None:
+        for r, c in enumerate(cores):
+            if helper_of(c, topo) == core:
+                far = [cores[(r - 1 - t) % n] for t in range(NR)]
+                g.wait_ge(T.sem.hin, count(topo.mask(c, core) & ~topo.mask(c, far[0])))
+                total = 0
+                for t in range(NR):
+                    m = topo.mask(core, far[t])
+                    send(g, T, topo, core, far[t], T["wr%dc" % t][:, 256:512].bitcast(dt.uint8),
+                         T.hand[:, 0:256].bitcast(dt.uint8), "w%d" % t, m)
+                    total += count(m)
+                g.wait_ge(T.sem.sent, total)
+        return
+
+    ops = []
+
+    def V(name, a=None, b=None, step=1):
+        if a is None:
+            a, b = 0, SCRATCH[name][1][1]
+        cols = 0
+        for c in range(a, b, step):
+            cols |= 1 << c
+        last = a + (len(range(a, b, step)) - 1) * step + 1
+        return (T[name][:, a:last:step] if step > 1 else T[name][:, a:b], name, cols)
+
+    def op(q, name, fn, r, w, grp=None, dma=False, after=(), sem=None):
+        ops.append({"q": q, "name": name, "fn": fn, "r": [x for x in r if isinstance(x, tuple)], "w": list(w),
+                    "grp": grp, "dma": dma, "after": list(after), "sem": sem})
+        return len(ops) - 1
+
+    def ap(x):
+        return x[0] if isinstance(x, tuple) else x
+
+    def ts(out, in0, s1, o0, s2=None, o1=None, grp=None):
+        if o1 is None:
+            return op("v", "ts " + out[1], lambda e: e.tensor_scalar(out[0], in0[0], ap(s1), None, o0), [in0, s1], [out], grp)
+        return op("v", "ts " + out[1], lambda e: e.tensor_scalar(out[0], in0[0], ap(s1), ap(s2), o0, o1),
+                  [in0, s1, s2], [out], grp)
+
+    def tt(out, in0, in1, o, off=None, grp=None):
+        if off is None:
+            return op("v", "tt " + out[1], lambda e: e.tensor_tensor(out[0], in0[0], in1[0], o), [in0, in1], [out], grp)
+        return op("v", "tti " + out[1], lambda e: e.tensor_tensor(out[0], in0[0].indirect(off[0]), in1[0], o),
+                  [in0, in1, off], [out], grp)
+
+    def cp(out, in_, off=None, grp=None):
+        if off is None:
+            return op("v", "cp " + out[1], lambda e: e.tensor_copy(out[0], in_[0]), [in_], [out], grp)
+        return op("v", "cpi " + out[1], lambda e: e.tensor_copy(out[0], in_[0].indirect(off[0])), [in_, off], [out], grp)
+
+    def fill(out, c, grp=None):
+        return op("v", "fill " + out[1], lambda e: e.memset(out[0], c), [], [out], grp)
+
+    def scan(out, d0, d1, init, o0, o1):
+        return op("v", "scan " + out[1], lambda e: e.tensor_tensor_scan(out[0], d0[0], d1[0], ap(init), o0, o1),
+                  [d0, d1, init], [out])
+
+    def turn(out, in_, grp=None):
+        return op("v", "turn " + out[1], lambda e: e.transpose(out[0], in_[0]), [in_], [out], grp)
+
+    def total(out, in_):
+        return op("v", "sum " + out[1], lambda e: e.tensor_reduce(out[0], in_[0], AxisListType.X, A.add), [in_], [out])
+
+    def act(out, in_, off=None, scale=None, grp=None):
+        if off is not None:
+            return op("s", "acti " + out[1], lambda e: e.activation(out[0], in_[0].indirect(off[0]), AF.Copy),
+                      [in_, off], [out], grp)
+        if scale is not None:
+            return op("s", "acts " + out[1], lambda e: e.activation(out[0], in_[0], AF.Copy, scale=scale), [in_], [out], grp)
+        return op("s", "act " + out[1], lambda e: e.activation(out[0], in_[0], AF.Copy), [in_], [out], grp)
+
+    def line(out, in_, func, bias, scale, grp=None):
+        return op("s", "line " + out[1], lambda e: e.activation(out[0], in_[0], func, bias=ap(bias), scale=scale),
+                  [in_, bias], [out], grp)
+
+    def quant(q, a, b, in_, grp=None):
+        c, s = V(q + "c", a, b), V(q + "s", a, b)
+        return op("v", "quant " + q, lambda e: e.quantize_mx(c[0], s[0], in_[0]), [in_], [c, s], grp)
+
+    def mm(bank, w, wa, x, a, b):
+        out, wc, ws = V("ps%d" % bank, 0, b - a), V(w + "c", wa, wa + 128), V(w + "s", wa, wa + 128)
+        xc, xs = V(x + "c", a, b), V(x + "s", a, b)
+        return op("p", "mm " + w + x, lambda e: e.matmul_mx(out[0], wc[0], ws[0], xc[0], xs[0], True, True),
+                  [wc, ws, xc, xs], [out])
+
+    def pick(dst, src, off, a=None, b=None):
+        oc, ic, os_, is_ = V(dst + "c", a, b), V(src + "c"), V(dst + "s", a, b), V(src + "s")
+        op("v", "pick " + dst, lambda e: e.tensor_copy(oc[0].bitcast(dt.uint32), ic[0].bitcast(dt.uint32).indirect(off[0])),
+           [ic, off], [oc])
+        act(os_, is_, off)
+
+    def iota(out, pattern, base, cm, exact=False):
+        if exact:
+            return op("g", "iota " + out[1], lambda e: e.iota(out[0], pattern, base, cm), [], [out])
+        return op("g", "iota " + out[1],
+                  lambda e: e.iota(out[0], pattern, base, cm, allow_small_or_imprecise_dtypes=True), [], [out])
+
+    def dma(q, out, in_, r, w, grp=None, after=()):
+        return op(q, "dma", lambda e: e.dma_start(out, in_), r, w, grp, True, after)
+
+    def bytes_of(v):
+        return v[0].bitcast(dt.uint8)
+
+    dma("y", bytes_of(V("wlc", 256, 512)), T.wc[:, 1024:2048], [], [V("wlc", 256, 512)])
+    dma("s", T.xt[:, 0:960], T.x[:, 0:960], [], [V("xt", 0, 960)])
+    dma("y", T.xt[:, 960:1920], T.x[:, 960:1920], [], [V("xt", 960, 1920)])
+    dma("s", T.ut[:], T.u[:], [], [V("ut")])
+    lw = dma("y", bytes_of(V("wlc", 0, 256)), T.wc[:, 0:1024], [], [V("wlc", 0, 256)])
+    dma("s", T.wls[:], T.ws[:], [], [V("wls")])
+    dma("y", T.vt[:], T.v[:], [], [V("vt")], after=[lw])
+
+    iota(V("pi", 0, 1), [[0, 1]], 0, 1, True)
+    iota(V("kr"), [[1, 48]], -1, 0)
+    iota(V("j16"), [[16, 32]], 0, 0)
+    iota(V("zi"), [[1, 520]], -2, -4)
+    far = [cores[(rank - 1 - t) % n] for t in range(NR)]
+    hp = helper_of(core, topo)
+    out_mask = topo.mask(core, far[0])
+    on_mask = topo.mask(core, hp) & ~out_mask
+    sent = [0]
+
+    def remote(dst, out, in_, src, sem, mask):
+        op("g", "remote", lambda e: send(e, T, topo, core, dst, out, in_, sem, mask), [src], [])
+        sent[0] += count(mask)
+
+    remote(hp, T.hand[:, 0:256].bitcast(dt.uint8), bytes_of(V("wlc", 256, 512)), V("wlc", 256, 512), "hin", on_mask)
+    iota(V("vals"), [[1, C]], 0, 0)
+    for t in range(NR):
+        m = topo.mask(core, far[t])
+        remote(far[t], T["wr%dc" % t][:, 0:256].bitcast(dt.uint8), bytes_of(V("wlc", 0, 256)), V("wlc", 0, 256), "w%d" % t, m)
+        remote(far[t], T["wr%ds" % t][:], T.wls[:], V("wls"), "w%d" % t, m)
+        giver = cores[(rank + 1 + t) % n]
+        arrivals = 2 * count(topo.mask(giver, core)) + count(topo.mask(helper_of(giver, topo), core))
+        op(None, "arrive", None, [], [V("wr%dc" % t), V("wr%ds" % t)], sem=("w%d" % t, arrivals))
+
+    def col(k):
+        return V("cf", k, k + 1)
+
+    ci, o16, par, low, p32 = col(0), col(1), col(4), col(5), col(6)
+    c30, parc, kin, cc, half = col(8), col(9), col(10), col(11), col(12)
+    pi = V("pi", 0, 1)
+    fill(V("ge"), 0.0)
+    fill(V("caps"), -BIG, "f0")
+    fill(V("d0"), -1.0, "f0")
+    fill(V("pat"), 1.0)
+    fill(V("ta", ODD + 64, ODD + 96), 0.0, "f0")
+    fill(V("ta", ODD + 576, ODD + 608), 0.0, "f0")
+    ts(V("ci", 2, 3), pi, 4, A.arith_shift_right)
+    ts(V("ci", 0, 1), pi, 15, A.bitwise_and, grp="i0")
+    ts(V("ci", 1, 2), pi, 16, A.bitwise_and, grp="i0")
+    tt(V("ci", 3, 4), V("ci", 2, 3), pi, A.add)
+    ts(V("ci", 5, 6), pi, 1, A.bitwise_and, grp="i0")
+    ts(V("ci", 6, 7), pi, 31, A.bitwise_and, grp="i0")
+    ts(V("ci", 4, 5), V("ci", 3, 4), 1, A.bitwise_and, grp="i0")
+    fill(V("fs", C, 4 * FW, FW), 0.0)
+    cp(V("cf", 0, 7), V("ci", 0, 7))
+    fill(V("pat", 0, 155, 5), 0.0)
+    ts(c30, ci, float(BLK), A.mult, grp="i1")
+    ts(parc, par, -688.0, A.mult, float(ODD), A.add, grp="i1")
+    ts(V("bl", 0, 3), V("j16", 0, 3), ci, A.add, grp="i1")
+    ts(half, ci, 15.0, A.is_lt, 0.5, A.subtract, grp="i1")
+    ts(V("d0", 0, 4), V("d0", 0, 4), ci, A.mult, -1.0, A.max)
+    ts(V("fore"), V("kr", 0, 32), c30, A.add, float(C - 1), A.min)
+    ts(V("bl", 4, 7), V("bl", 0, 3), 4.0, A.is_ge, 32.0, A.mult, grp="i2")
+    ts(V("bl", 8, 11), V("bl", 0, 3), 34.0, A.is_ge, 32.0, A.mult, grp="i2")
+    ts(V("bl", 12, 15), V("bl", 0, 3), 16.0, A.mult, parc, A.add, grp="i2")
+    ts(V("caps", 34, 38), V("caps", 34, 38), half, A.mult)
+    ts(V("msk", 32, 64), V("kr", 1, 33), p32, A.is_gt, grp="i4")
+    ts(V("msk", 64, 96), V("kr", 1, 33), o16, A.subtract, 15.0, A.is_le, grp="i4")
+    for b in range(2):
+        ts(V("et", 528 * b, 528 * b + 520), V("zi"), float(b), A.is_equal)
+    for t in range(NR):
+        line(V("er%d" % t, 0, DW), V("zi", 0, DW), AF.Identity, float(C), 0.0)
+    tt(V("bl", 16, 19), V("bl", 4, 7), V("bl", 8, 11), A.add)
+    ts(kin, c30, o16, A.subtract, 511.0, A.add, grp="i3")
+    ts(col(13), ci, 15.0, A.mult, o16, A.subtract, grp="i3")
+    tt(V("bl", 20, 23), V("bl", 16, 19), V("bl", 12, 15), A.add)
+    for b in range(4):
+        a = 528 * (b % 2) + 2 - 2 * (b // 2)
+        quant("qe", 128 * b, 128 * b + 128, V("et", a, a + 512), "qe")
+    for t in range(NR):
+        ts(V("boff", 4 * t, 4 * t + 3), V("bl", 20, 23), float(t), A.add, float(TAW - 1), A.min, grp="bo")
+    ts(col(14), col(13), 526.0, A.add, ci, A.mult)
+    ts(V("kt", 0, BLK), V("kr", 1, BLK + 1), kin, A.add, 2.0, A.add)
+    tt(V("msk", 0, 32), V("msk", 32, 64), V("msk", 64, 96), A.mult)
+    ts(cc, col(14), -1.0, A.mult, o16, A.add)
+
+    quant("qx", 0, 240, V("xt", 0, 960), "qx")
+    quant("qx", 240, C, V("xt", 960, 1920), "qx")
+    pick("qa", "qx", V("fore"))
+    quant("qu", 0, 128, V("ut"))
+
+    ones = V("pat", 1, 150, 5)
+    mask = V("msk", 0, 32)
+    stores = []
+    for t in range(NR):
+        q, er, pt, ht, qp, qh = "q" + "ab"[t], "er%d" % t, "pt%d" % t, "ht%d" % t, "qp%d" % t, "qh%d" % t
+        G = lambda s: s + str(t)
+        mm(4, "qu", 0, q, 0, 512)
+        for b in range(4):
+            mm(b, "qe", 128 * b, q, 16, 16 + C)
+        if t == 0:
+            ts(col(16), ci, 16.0, A.mult, o16, A.add)
+            ts(V("sg", 0, 155, 5), V("kr", 2, 33), 2.0, A.mult)
+            ts(col(17), low, 144.0, A.mult, col(16), A.add)
+            ts(V("up", 0, BLK), V("j16", 0, BLK), ci, A.add)
+            ts(V("ew", 0, 1), col(17), 319.0, A.min)
+        else:
+            quant("qv", 0, 128, V("vt"))
+            ts(V("up", 32, 32 + BLK), V("up", 0, BLK), -14.5, A.add, 1.0 / BLK, A.mult)
+            ts(V("up", 64, 64 + BLK), V("up", 0, BLK), 16.0, A.mult)
+            cp(V("ai", 0, BLK), V("up", 32, 32 + BLK))
+        for b in range(4):
+            act(V("fs", FW * b, FW * b + C), V("ps%d" % b, 0, C))
+        for a, b, o in ((0, 512, 96), (16, 496, ODD + 96), (415, 511, 0), (431, 495, ODD), (1, 97, 608), (17, 81, ODD + 608)):
+            turn(V("ta", o, o + b - a), V("ps4", a, b), G("ta"))
+        tt(V("bb"), V("ta"), V("caps"), A.max, V("boff", 4 * t, 4 * t + 3))
+        for k in range(1, 5):
+            w = 38 - k
+            tt(V("ge", 5 - k, 5 * w, 5), V("bb", k, k + w), V("bb", 0, w), A.is_ge, grp=G("ge"))
+        scan(V("rl", 0, 185), V("ge", 0, 185), V("ge", 0, 185), 0.0, A.mult, A.add)
+        scan(V("dd", 0, 37), V("d0", 0, 37), V("rl", 4, 185, 5), 4.0, A.add, A.max)
+        for e in range(4):
+            line(V("sg", 1 + e, 155, 5), V("dd", 3 + e, 34 + e), AF.Sign, 3.5 - e, -1.0, G("sg"))
+        hit = V("hit", 0, BLK)
+        tt(hit, V("dd", 4, 34), V("dd", 3, 33), A.is_ge)
+        scan(V("u2", 0, BLK), ones, hit, kin, A.add, A.add)
+        tt(V("hk", 0, BLK), hit, V("kt", 0, BLK), A.mult)
+        ts(V("xx"), mask, V("u2", BLK - 1, BLK), A.mult)
+        tt(V("apr", 0, BLK), V("u2", 0, BLK), V("hk", 0, BLK), A.subtract)
+        turn(V("yy"), V("xx"))
+        total(V("bs", 0, 1), V("yy"))
+        ts(V("pos", 0, BLK), V("apr", 0, BLK), V("bs", 0, 1), A.add, cc, A.add)
+        scan(V("m2", 0, 155), V("pat", 0, 155), V("sg", 0, 155), 0.0, A.mult, A.add)
+        win, off, val = V(er), V("pos", 0, BLK), V("vals")
+        op("v", "scatter", lambda e, win=win, off=off, val=val: e.tensor_copy(win[0].indirect(off[0]), val[0]), [off, val], [win])
+        tt(V("nw", 0, BLK), V("m2", 9, 155, 5), V("m2", 4, 150, 5), A.not_equal)
+        turn(V("tb", 0, CAP), V(er, 0, CAP), G("tb"))
+        turn(V("tb", CAP, 2 * CAP), V(er, 16, 16 + CAP), G("tb"))
+        scan(V("un", 0, BLK), ones, V("nw", 0, BLK), 0.0, A.mult, A.add)
+        cp(V("eoff"), V("tb"), V("ew", 0, 1))
+        ts(V("x2"), mask, V("un", BLK - 1, BLK), A.mult)
+        for b in range(2):
+            cp(V(pt, b, 4 * CAP, 4), V("fs", FW * b, FW * b + C + 1), V("eoff", 0, 10), G("pv"))
+            act(V(pt, b + 2, 4 * CAP, 4), V("fs", FW * (b + 2), FW * (b + 2) + C + 1), V("eoff", 0, 10), grp=G("pa"))
+        turn(V("y2"), V("x2"))
+        quant(qp, 0, CAP, V(pt))
+        for b in (0, 2, 1, 3):
+            mm(4 + b, "wr%d" % t, 128 * b, qp, 0, CAP)
+        total(V("bs", 4, 5), V("y2"))
+        if t == 0:
+            fill(V("dh", 0, 4 * DW, DW), 0.0, "f1")
+            fill(V("dh", CAP + 1, 4 * DW, DW), 0.0, "f1")
+        else:
+            ts(V("up", 96, 96 + BLK), V("ai", 0, BLK), -float(C - 1), A.mult)
+        noff = V("noff", 0, BLK)
+        ts(noff, V("un", 0, BLK), V("bs", 4, 5), A.add, float(CAP + 1), A.min)
+        for b in range(2):
+            ts(V(ht, b, 4 * CAP, 4), V("ps%d" % (4 + b), 0, CAP), 0.03125, A.mult, grp=G("hv"))
+            act(V(ht, b + 2, 4 * CAP, 4), V("ps%d" % (6 + b), 0, CAP), scale=0.03125, grp=G("ha"))
+        quant(qh, 0, CAP, V(ht))
+        for b in (0, 2, 1, 3):
+            mm(4 + b, "qe", 128 * b, qh, 0, CAP)
+        if t == 0:
+            fill(V("t1", 0, 64), 0.0, "f2")
+            fill(V("t1", 1984, 2048), 0.0, "f2")
+        else:
+            ts(V("nf", 0, BLK), V("un", 0, BLK), V("bs", 4, 5), A.add, -1.0, A.add)
+            tt(V("up", 32, 32 + BLK), V("up", 96, 96 + BLK), V("up", 64, 64 + BLK), A.add)
+            line(V("mf", 0, BLK), V("m2", 9, 155, 5), AF.Identity, c30, 0.5)
+            stores.append(dma("y", T.ol[:, C:2 * C], T.nf[:, 0:BLK], [V("nf", 0, BLK)], [], "ol"))
+            stores.append(dma("y", T.ol[:, 0:C], T.mf[:, 0:BLK], [V("mf", 0, BLK)], [], "ol"))
+        new, o = ("t1", 64) if t < NR - 1 else ("t2", 0)
+        for b in range(2):
+            cp(V("dh", DW * b + 1, DW * b + 1 + CAP), V("ps%d" % (4 + b), 0, CAP))
+            act(V("dh", DW * (b + 2) + 1, DW * (b + 2) + 1 + CAP), V("ps%d" % (6 + b), 0, CAP))
+        for b in range(2):
+            tt(V(new, o + b, o + 4 * C, 4), V("dh", DW * b, DW * b + CAP + 2), V("fs", FW * b, FW * b + C), A.add, noff, G("tn"))
+            act(V("gg", C * b, C * b + C), V("dh", DW * (b + 2), DW * (b + 2) + CAP + 2), noff)
+        for b in range(2):
+            tt(V(new, o + 2 + b, o + 4 * C, 4), V("gg", C * b, C * b + C), V("ps%d" % (2 + b), 0, C), A.add, grp=G("tn"))
+        if t < NR - 1:
+            quant("qb", 0, 512, V("t1"))
+        else:
+            cp(V("back", 0, BLK), V("up", 32, 32 + BLK))
+            quant("qy", 0, C, V("t2"))
+
+    for h, (a, b) in enumerate(((0, 256), (256, C))):
+        pick("qz", "qy", V("back", a // 16, b // 16), a, b)
+        mm(4 + h, "qv", 0, "qz", a, b)
+        stores.append(dma("y", T.oc[:, 4 * a:4 * b], bytes_of(V("qzc", a, b)), [V("qzc", a, b)], [], "out"))
+    for k in range(4):
+        stores.append(dma("y", T.osc[4 * k:4 * k + 4, :], T.qzs[32 * k:32 * k + 4, :], [V("qzs")], [], "out"))
+    cp(V("ysb", 0, 256), V("ps4", 0, 256))
+    act(V("ysb", 256, C), V("ps5", 0, C - 256))
+    stores.append(dma("y", T.y[:, 0:256], T.ysb[:, 0:256], [V("ysb", 0, 256)], [], "out"))
+    stores.append(dma("s", T.y[:, 256:C], T.ysb[:, 256:C], [V("ysb", 256, C)], [], "out"))
+    op("y", "end", None, [], [], after=stores)
+    plan(g, T, ops)
+    g.wait_ge(T.sem.sent, sent[0])

@@ -1,11 +1,14 @@
 from concourse.mybir import dt, AluOpType as A, AxisListType, ActivationFunctionType as AF
 
 C, CAP, NR = 480, 160, 2
-BLK = C // 16
+BLK = 32
 FW, DW = 496, 176
-TAW, ODD = 1376, 704
-EWID = 1472
-BIG = 9e29
+SL = 2 * (CAP + 16)
+SPARE = 1100
+EWID = 2560
+BIG = 4.5e29
+RUNS = ((0, 256), (256, C))
+LAST = ((0, 320), (320, C))
 
 F32, BF, I32, U16, X4, U8 = "float32", "bfloat16", "int32", "uint16", "float8_e4m3fn_x4", "uint8"
 SCRATCH = {}
@@ -15,25 +18,24 @@ def _sb(name, n, d):
     SCRATCH[name] = ("sbuf", [128, n], d)
 
 
-for _n, _w in (("wl", 512), ("wr0", 512), ("wr1", 512), ("qu", 128), ("qv", 128), ("qe", 512), ("qx", C), ("qa", 512),
-               ("qb", 512), ("qy", C), ("qz", C), ("qp0", CAP), ("qp1", CAP), ("qh0", CAP), ("qh1", CAP)):
+for _n, _w in (("wl", 512), ("wr0", 512), ("wr1", 512), ("qu", 128), ("qv", 128), ("qe", 512), ("qa", C),
+               ("qb", C), ("qy", C), ("qp0", CAP), ("qp1", CAP), ("qh0", CAP), ("qh1", CAP)):
     _sb(_n + "c", _w, X4)
     _sb(_n + "s", _w, U8)
 _sb("hand", 256, X4)
-for _n, _w in (("xt", 4 * C), ("ut", 512), ("vt", 512), ("zi", 520), ("et", 1056), ("t1", 2048), ("t2", 4 * C),
-               ("fs", 4 * FW), ("dh", 4 * DW), ("gg", 2 * C), ("pt0", 4 * CAP), ("pt1", 4 * CAP), ("ht0", 4 * CAP),
-               ("ht1", 4 * CAP), ("ge", 192), ("rl", 192), ("sg", 160), ("pat", 160), ("m2", 160)):
+for _n, _w in (("xt", 4 * C), ("ut", 512), ("vt", 512), ("zi", 520), ("et", 1056), ("t1", 4 * C), ("t2", 4 * C),
+               ("fs", 4 * FW), ("dh", 4 * DW), ("gg", 3 * C), ("pt0", 4 * CAP), ("pt1", 4 * CAP), ("ht0", 4 * CAP),
+               ("ht1", 4 * CAP), ("ge", 200), ("rl", 200), ("sg", 168), ("pat", 168), ("m2", 168)):
     _sb(_n, _w, BF)
-for _n, _w in (("kr", 48), ("j16", 32), ("vals", C), ("cf", 32), ("bl", 32), ("msk", 96), ("kt", 32), ("d0", 40),
-               ("caps", 48), ("er0", EWID), ("er1", EWID), ("ta", TAW), ("bb", 48),
-               ("dd", 40), ("hit", 32), ("u2", 32), ("hk", 32), ("xx", 32), ("apr", 32), ("yy", 32), ("bs", 8),
-               ("tb", 320), ("nw", 32), ("un", 32), ("x2", 32), ("y2", 32), ("mf", 32), ("nf", 32),
-               ("up", 128), ("ysb", C)):
+for _n, _w in (("kr", 48), ("j16", 32), ("vals", 256), ("cf", 32), ("bl", 32), ("msk", 96), ("zz", 16), ("d0", 40),
+               ("er0", EWID), ("er1", EWID), ("alt", SL), ("es", SL), ("ta", 488), ("xg", 96), ("bb", 96),
+               ("dd", 40), ("nh", 40), ("u2", 40), ("hb", 16), ("hc", 16), ("sw", 16), ("xx", 32), ("apr", 16),
+               ("yy", 32), ("bs", 8), ("tb", 320), ("nw", 32), ("un", 32), ("x2", 32), ("y2", 32), ("mf", 32),
+               ("nf", 32), ("nb", 48), ("tn", 64), ("ysb", C)):
     _sb(_n, _w, F32)
 _sb("pi", 8, I32)
 _sb("ci", 8, I32)
-_sb("ai", 32, I32)
-for _n, _w in (("fore", 32), ("back", 32), ("boff", 8), ("ew", 2), ("pos", 32), ("eoff", 16), ("noff", 32)):
+for _n, _w in (("boff", 12), ("ew", 2), ("nof", 2), ("pos", 16), ("eoff", 16), ("noff", 32)):
     _sb(_n, _w, U16)
 for _b in range(8):
     SCRATCH["ps%d" % _b] = ("psum", [128, 512], F32)
@@ -177,6 +179,10 @@ def rank_program(g, core, T, topo):
         return op("v", "ts " + out[1], lambda e: e.tensor_scalar(out[0], in0[0], ap(s1), ap(s2), o0, o1),
                   [in0, s1, s2], [out], grp)
 
+    def tsi(out, in0, off, s1, o0):
+        return op("v", "tsi " + out[1], lambda e: e.tensor_scalar(out[0], in0[0].indirect(off[0]), s1, None, o0),
+                  [in0, off], [out])
+
     def tt(out, in0, in1, o, off=None, grp=None):
         if off is None:
             return op("v", "tt " + out[1], lambda e: e.tensor_tensor(out[0], in0[0], in1[0], o), [in0, in1], [out], grp)
@@ -223,12 +229,6 @@ def rank_program(g, core, T, topo):
         return op("p", "mm " + w + x, lambda e: e.matmul_mx(out[0], wc[0], ws[0], xc[0], xs[0], True, True),
                   [wc, ws, xc, xs], [out])
 
-    def pick(dst, src, off, a=None, b=None):
-        oc, ic, os_, is_ = V(dst + "c", a, b), V(src + "c"), V(dst + "s", a, b), V(src + "s")
-        op("v", "pick " + dst, lambda e: e.tensor_copy(oc[0].bitcast(dt.uint32), ic[0].bitcast(dt.uint32).indirect(off[0])),
-           [ic, off], [oc])
-        act(os_, is_, off)
-
     def iota(out, pattern, base, cm, exact=False):
         if exact:
             return op("g", "iota " + out[1], lambda e: e.iota(out[0], pattern, base, cm), [], [out])
@@ -241,18 +241,19 @@ def rank_program(g, core, T, topo):
     def bytes_of(v):
         return v[0].bitcast(dt.uint8)
 
+    dma("s", T.xt[:, 0:1024], T.x[:, 0:1024], [], [V("xt", 0, 1024)])
+    dma("y", T.ut[:], T.u[:], [], [V("ut")])
+    dma("s", T.xt[:, 1024:1920], T.x[:, 1024:1920], [], [V("xt", 1024, 1920)])
     dma("y", bytes_of(V("wlc", 256, 512)), T.wc[:, 1024:2048], [], [V("wlc", 256, 512)])
-    dma("s", T.xt[:, 0:960], T.x[:, 0:960], [], [V("xt", 0, 960)])
-    dma("y", T.xt[:, 960:1920], T.x[:, 960:1920], [], [V("xt", 960, 1920)])
-    dma("s", T.ut[:], T.u[:], [], [V("ut")])
     lw = dma("y", bytes_of(V("wlc", 0, 256)), T.wc[:, 0:1024], [], [V("wlc", 0, 256)])
     dma("s", T.wls[:], T.ws[:], [], [V("wls")])
     dma("y", T.vt[:], T.v[:], [], [V("vt")], after=[lw])
 
     iota(V("pi", 0, 1), [[0, 1]], 0, 1, True)
+    iota(V("zi"), [[1, 520]], -2, -4)
     iota(V("kr"), [[1, 48]], -1, 0)
     iota(V("j16"), [[16, 32]], 0, 0)
-    iota(V("zi"), [[1, 520]], -2, -4)
+    iota(V("vals"), [[2, 16], [BLK, 16]], 0, 0)
     far = [cores[(rank - 1 - t) % n] for t in range(NR)]
     hp = helper_of(core, topo)
     out_mask = topo.mask(core, far[0])
@@ -264,7 +265,6 @@ def rank_program(g, core, T, topo):
         sent[0] += count(mask)
 
     remote(hp, T.hand[:, 0:256].bitcast(dt.uint8), bytes_of(V("wlc", 256, 512)), V("wlc", 256, 512), "hin", on_mask)
-    iota(V("vals"), [[1, C]], 0, 0)
     for t in range(NR):
         m = topo.mask(core, far[t])
         remote(far[t], T["wr%dc" % t][:, 0:256].bitcast(dt.uint8), bytes_of(V("wlc", 0, 256)), V("wlc", 0, 256), "w%d" % t, m)
@@ -277,14 +277,16 @@ def rank_program(g, core, T, topo):
         return V("cf", k, k + 1)
 
     ci, o16, par, low, p32 = col(0), col(1), col(4), col(5), col(6)
-    c30, parc, kin, cc, half = col(8), col(9), col(10), col(11), col(12)
+    c32, o32 = col(8), col(9)
     pi = V("pi", 0, 1)
-    fill(V("ge"), 0.0)
-    fill(V("caps"), -BIG, "f0")
+    fill(V("ge"), 0.0, "f0")
     fill(V("d0"), -1.0, "f0")
     fill(V("pat"), 1.0)
-    fill(V("ta", ODD + 64, ODD + 96), 0.0, "f0")
-    fill(V("ta", ODD + 576, ODD + 608), 0.0, "f0")
+    fill(V("ta", C, C + 8), BIG, "f0")
+    fill(V("nh", 0, 1), 1.0, "f0")
+    fill(V("fs", C, 4 * FW, FW), 0.0, "f0")
+    fill(V("alt", 0, SL, 2), 0.0, "f0")
+    fill(V("alt", 1, SL, 2), 1.0, "f0")
     ts(V("ci", 2, 3), pi, 4, A.arith_shift_right)
     ts(V("ci", 0, 1), pi, 15, A.bitwise_and, grp="i0")
     ts(V("ci", 1, 2), pi, 16, A.bitwise_and, grp="i0")
@@ -292,93 +294,84 @@ def rank_program(g, core, T, topo):
     ts(V("ci", 5, 6), pi, 1, A.bitwise_and, grp="i0")
     ts(V("ci", 6, 7), pi, 31, A.bitwise_and, grp="i0")
     ts(V("ci", 4, 5), V("ci", 3, 4), 1, A.bitwise_and, grp="i0")
-    fill(V("fs", C, 4 * FW, FW), 0.0)
+    fill(V("pat", 0, 165, 5), 0.0)
     cp(V("cf", 0, 7), V("ci", 0, 7))
-    fill(V("pat", 0, 155, 5), 0.0)
-    ts(c30, ci, float(BLK), A.mult, grp="i1")
-    ts(parc, par, -688.0, A.mult, float(ODD), A.add, grp="i1")
-    ts(V("bl", 0, 3), V("j16", 0, 3), ci, A.add, grp="i1")
-    ts(half, ci, 15.0, A.is_lt, 0.5, A.subtract, grp="i1")
-    ts(V("d0", 0, 4), V("d0", 0, 4), ci, A.mult, -1.0, A.max)
-    ts(V("fore"), V("kr", 0, 32), c30, A.add, float(C - 1), A.min)
-    ts(V("bl", 4, 7), V("bl", 0, 3), 4.0, A.is_ge, 32.0, A.mult, grp="i2")
-    ts(V("bl", 8, 11), V("bl", 0, 3), 34.0, A.is_ge, 32.0, A.mult, grp="i2")
-    ts(V("bl", 12, 15), V("bl", 0, 3), 16.0, A.mult, parc, A.add, grp="i2")
-    ts(V("caps", 34, 38), V("caps", 34, 38), half, A.mult)
-    ts(V("msk", 32, 64), V("kr", 1, 33), p32, A.is_gt, grp="i4")
-    ts(V("msk", 64, 96), V("kr", 1, 33), o16, A.subtract, 15.0, A.is_le, grp="i4")
+    fill(V("dh", 0, 4 * DW, DW), 0.0, "f1")
+    fill(V("dh", CAP + 1, 4 * DW, DW), 0.0, "f1")
     for b in range(2):
         ts(V("et", 528 * b, 528 * b + 520), V("zi"), float(b), A.is_equal)
     for t in range(NR):
-        line(V("er%d" % t, 0, DW), V("zi", 0, DW), AF.Identity, float(C), 0.0)
-    tt(V("bl", 16, 19), V("bl", 4, 7), V("bl", 8, 11), A.add)
-    ts(kin, c30, o16, A.subtract, 511.0, A.add, grp="i3")
-    ts(col(13), ci, 15.0, A.mult, o16, A.subtract, grp="i3")
-    tt(V("bl", 20, 23), V("bl", 16, 19), V("bl", 12, 15), A.add)
+        line(V("er%d" % t, 0, SL), V("zi", 0, SL), AF.Identity, -100.0, 0.0)
+    ts(c32, ci, float(BLK), A.mult, grp="i1")
+    ts(o32, o16, 2.0, A.mult, grp="i1")
+    ts(col(10), ci, 16.0, A.mult, o16, A.add, grp="i1")
+    ts(col(11), par, 32.0, A.mult, o16, A.add, grp="i1")
+    ts(col(12), ci, low, A.subtract, 0.5, A.mult, grp="i1")
+    ts(V("d0", 0, 4), V("d0", 0, 4), ci, A.mult, -1.0, A.max)
+    ts(V("msk", 32, 64), V("kr", 1, 33), p32, A.is_gt, grp="i4")
+    ts(V("msk", 64, 96), V("kr", 1, 33), o16, A.subtract, 15.0, A.is_le, grp="i4")
     for b in range(4):
         a = 528 * (b % 2) + 2 - 2 * (b // 2)
         quant("qe", 128 * b, 128 * b + 128, V("et", a, a + 512), "qe")
     for t in range(NR):
-        ts(V("boff", 4 * t, 4 * t + 3), V("bl", 20, 23), float(t), A.add, float(TAW - 1), A.min, grp="bo")
-    ts(col(14), col(13), 526.0, A.add, ci, A.mult)
-    ts(V("kt", 0, BLK), V("kr", 1, BLK + 1), kin, A.add, 2.0, A.add)
+        ts(V("bl", 6 * t, 6 * t + 6), V("j16", 0, 6), c32, A.add, float(t - BLK), A.add, grp="i2")
+    ts(col(13), low, 144.0, A.mult, col(10), A.add, grp="i2")
+    ts(V("bl", 16, 18), V("j16", 0, 2), 0.5, A.mult, col(11), A.add, grp="i2")
+    ts(V("zz"), V("kr", 1, 17), col(10), A.add, float(SPARE), A.add, grp="i2")
     tt(V("msk", 0, 32), V("msk", 32, 64), V("msk", 64, 96), A.mult)
-    ts(cc, col(14), -1.0, A.mult, o16, A.add)
+    ts(V("boff"), V("bl", 0, 12), 0.0, A.max, float(C), A.min)
 
-    quant("qx", 0, 240, V("xt", 0, 960), "qx")
-    quant("qx", 240, C, V("xt", 960, 1920), "qx")
-    pick("qa", "qx", V("fore"))
     quant("qu", 0, 128, V("ut"))
+    for h, (a, b) in enumerate(RUNS):
+        quant("qa", a, b, V("xt", 4 * a, 4 * b))
+        mm(4 + h, "qu", 0, "qa", a, b)
+        if h == 0:
+            ts(V("ew", 0, 1), col(13), 319.0, A.min)
+            ts(V("nof"), V("bl", 16, 18), col(12), A.add)
+            ts(V("sg", 0, 165, 5), V("kr", 2, 35), 2.0, A.mult)
 
-    ones = V("pat", 1, 150, 5)
+    ones = V("pat", 1, 165, 5)
+    ones32 = V("pat", 1, 160, 5)
     mask = V("msk", 0, 32)
     stores = []
     for t in range(NR):
         q, er, pt, ht, qp, qh = "q" + "ab"[t], "er%d" % t, "pt%d" % t, "ht%d" % t, "qp%d" % t, "qh%d" % t
+        final = t == NR - 1
         G = lambda s: s + str(t)
-        mm(4, "qu", 0, q, 0, 512)
         for b in range(4):
-            mm(b, "qe", 128 * b, q, 16, 16 + C)
-        if t == 0:
-            ts(col(16), ci, 16.0, A.mult, o16, A.add)
-            ts(V("sg", 0, 155, 5), V("kr", 2, 33), 2.0, A.mult)
-            ts(col(17), low, 144.0, A.mult, col(16), A.add)
-            ts(V("up", 0, BLK), V("j16", 0, BLK), ci, A.add)
-            ts(V("ew", 0, 1), col(17), 319.0, A.min)
-        else:
-            quant("qv", 0, 128, V("vt"))
-            ts(V("up", 32, 32 + BLK), V("up", 0, BLK), -14.5, A.add, 1.0 / BLK, A.mult)
-            ts(V("up", 64, 64 + BLK), V("up", 0, BLK), 16.0, A.mult)
-            cp(V("ai", 0, BLK), V("up", 32, 32 + BLK))
+            mm(b, "qe", 128 * b, q, 0, C)
         for b in range(4):
             act(V("fs", FW * b, FW * b + C), V("ps%d" % b, 0, C))
-        for a, b, o in ((0, 512, 96), (16, 496, ODD + 96), (415, 511, 0), (431, 495, ODD), (1, 97, 608), (17, 81, ODD + 608)):
-            turn(V("ta", o, o + b - a), V("ps4", a, b), G("ta"))
-        tt(V("bb"), V("ta"), V("caps"), A.max, V("boff", 4 * t, 4 * t + 3))
+        for h, (a, b) in enumerate(RUNS):
+            turn(V("ta", a, b), V("ps%d" % (4 + h), 0, b - a), G("ta"))
+        cp(V("xg"), V("ta", 0, C + 1), V("boff", 6 * t, 6 * t + 6))
+        turn(V("bb"), V("xg"))
         for k in range(1, 5):
-            w = 38 - k
-            tt(V("ge", 5 - k, 5 * w, 5), V("bb", k, k + w), V("bb", 0, w), A.is_ge, grp=G("ge"))
-        scan(V("rl", 0, 185), V("ge", 0, 185), V("ge", 0, 185), 0.0, A.mult, A.add)
-        scan(V("dd", 0, 37), V("d0", 0, 37), V("rl", 4, 185, 5), 4.0, A.add, A.max)
+            w = 40 - k
+            tt(V("ge", 5 - k, 5 * w, 5), V("bb", 28 + k, 28 + k + w), V("bb", 28, 28 + w), A.is_ge, grp=G("ge"))
+        scan(V("rl", 0, 195), V("ge", 0, 195), V("ge", 0, 195), 0.0, A.mult, A.add)
+        scan(V("dd", 0, 39), V("d0", 0, 39), V("rl", 4, 195, 5), 4.0, A.add, A.max)
         for e in range(4):
-            line(V("sg", 1 + e, 155, 5), V("dd", 3 + e, 34 + e), AF.Sign, 3.5 - e, -1.0, G("sg"))
-        hit = V("hit", 0, BLK)
-        tt(hit, V("dd", 4, 34), V("dd", 3, 33), A.is_ge)
-        scan(V("u2", 0, BLK), ones, hit, kin, A.add, A.add)
-        tt(V("hk", 0, BLK), hit, V("kt", 0, BLK), A.mult)
-        ts(V("xx"), mask, V("u2", BLK - 1, BLK), A.mult)
-        tt(V("apr", 0, BLK), V("u2", 0, BLK), V("hk", 0, BLK), A.subtract)
+            line(V("sg", 1 + e, 165, 5), V("dd", 3 + e, 36 + e), AF.Sign, 3.5 - e, -1.0, G("sg"))
+        tt(V("nh", 1, 33), V("dd", 4, 36), V("dd", 3, 35), A.is_lt)
+        scan(V("u2", 0, 33), ones, V("nh", 0, 33), 0.0, A.add, A.subtract)
+        tt(V("hb"), V("nh", 2, 33, 2), V("zz"), A.mult)
+        ts(V("xx"), mask, V("u2", 32, 33), A.mult, 2.0, A.mult)
+        tt(V("hc"), V("hb"), V("nh", 1, 33, 2), A.mult)
         turn(V("yy"), V("xx"))
+        tt(V("sw"), V("u2", 0, 32, 2), V("u2", 1, 33, 2), A.add)
         total(V("bs", 0, 1), V("yy"))
-        ts(V("pos", 0, BLK), V("apr", 0, BLK), V("bs", 0, 1), A.add, cc, A.add)
-        scan(V("m2", 0, 155), V("pat", 0, 155), V("sg", 0, 155), 0.0, A.mult, A.add)
-        win, off, val = V(er), V("pos", 0, BLK), V("vals")
+        tt(V("apr"), V("sw"), V("hc"), A.add)
+        ts(V("pos"), V("apr"), V("bs", 0, 1), A.add, o32, A.add)
+        win, off, val = V(er), V("pos"), V("vals")
         op("v", "scatter", lambda e, win=win, off=off, val=val: e.tensor_copy(win[0].indirect(off[0]), val[0]), [off, val], [win])
-        tt(V("nw", 0, BLK), V("m2", 9, 155, 5), V("m2", 4, 150, 5), A.not_equal)
-        turn(V("tb", 0, CAP), V(er, 0, CAP), G("tb"))
-        turn(V("tb", CAP, 2 * CAP), V(er, 16, 16 + CAP), G("tb"))
-        scan(V("un", 0, BLK), ones, V("nw", 0, BLK), 0.0, A.mult, A.add)
-        cp(V("eoff"), V("tb"), V("ew", 0, 1))
+        scan(V("m2", 0, 165), V("pat", 0, 165), V("sg", 0, 165), 0.0, A.mult, A.add)
+        scan(V("es"), V("alt"), V(er, 0, SL), -200.0, A.add, A.max)
+        tt(V("nw"), V("m2", 9, 165, 5), V("m2", 4, 160, 5), A.not_equal)
+        turn(V("tb", 0, CAP), V("es", 1, 2 * CAP, 2), G("tb"))
+        turn(V("tb", CAP, 2 * CAP), V("es", 33, SL, 2), G("tb"))
+        scan(V("un"), ones32, V("nw"), 0.0, A.mult, A.add)
+        tsi(V("eoff"), V("tb"), V("ew", 0, 1), float(C), A.min)
         ts(V("x2"), mask, V("un", BLK - 1, BLK), A.mult)
         for b in range(2):
             cp(V(pt, b, 4 * CAP, 4), V("fs", FW * b, FW * b + C + 1), V("eoff", 0, 10), G("pv"))
@@ -388,53 +381,54 @@ def rank_program(g, core, T, topo):
         for b in (0, 2, 1, 3):
             mm(4 + b, "wr%d" % t, 128 * b, qp, 0, CAP)
         total(V("bs", 4, 5), V("y2"))
-        if t == 0:
-            fill(V("dh", 0, 4 * DW, DW), 0.0, "f1")
-            fill(V("dh", CAP + 1, 4 * DW, DW), 0.0, "f1")
-        else:
-            ts(V("up", 96, 96 + BLK), V("ai", 0, BLK), -float(C - 1), A.mult)
-        noff = V("noff", 0, BLK)
-        ts(noff, V("un", 0, BLK), V("bs", 4, 5), A.add, float(CAP + 1), A.min)
+        ts(V("nb", 0, 32), V("un"), V("bs", 4, 5), A.add, grp=G("nb"))
+        ts(V("nb", 32, 48), V("un", 0, 16), V("bs", 4, 5), A.add, grp=G("nb"))
+        if final:
+            line(V("mf"), V("m2", 9, 165, 5), AF.Identity, c32, 0.5)
+            for k in range(8):
+                stores.append(dma("y", T.ol[k:k + 1, 0:C], T.mf[16 * k:16 * k + 15, :], [V("mf")], [], "ol"))
         for b in range(2):
             ts(V(ht, b, 4 * CAP, 4), V("ps%d" % (4 + b), 0, CAP), 0.03125, A.mult, grp=G("hv"))
             act(V(ht, b + 2, 4 * CAP, 4), V("ps%d" % (6 + b), 0, CAP), scale=0.03125, grp=G("ha"))
+        turn(V("tn", 0, 32), V("nb", 0, 32), G("tn"))
+        turn(V("tn", 32, 64), V("nb", 16, 48), G("tn"))
         quant(qh, 0, CAP, V(ht))
-        for b in (0, 2, 1, 3):
+        for b in (2, 0, 3, 1):
             mm(4 + b, "qe", 128 * b, qh, 0, CAP)
-        if t == 0:
-            fill(V("t1", 0, 64), 0.0, "f2")
-            fill(V("t1", 1984, 2048), 0.0, "f2")
+        tsi(V("noff"), V("tn"), V("nof"), float(CAP + 1), A.min)
+        if final:
+            ts(V("nf"), V("nb", 0, 32), -1.0, A.add)
+            for k in range(8):
+                stores.append(dma("y", T.ol[k:k + 1, C:2 * C], T.nf[16 * k:16 * k + 15, :], [V("nf")], [], "ol"))
         else:
-            ts(V("nf", 0, BLK), V("un", 0, BLK), V("bs", 4, 5), A.add, -1.0, A.add)
-            tt(V("up", 32, 32 + BLK), V("up", 96, 96 + BLK), V("up", 64, 64 + BLK), A.add)
-            line(V("mf", 0, BLK), V("m2", 9, 155, 5), AF.Identity, c30, 0.5)
-            stores.append(dma("y", T.ol[:, C:2 * C], T.nf[:, 0:BLK], [V("nf", 0, BLK)], [], "ol"))
-            stores.append(dma("y", T.ol[:, 0:C], T.mf[:, 0:BLK], [V("mf", 0, BLK)], [], "ol"))
-        new, o = ("t1", 64) if t < NR - 1 else ("t2", 0)
+            quant("qv", 0, 128, V("vt"))
+        new, qn = ("t2", "qy") if final else ("t1", "qb")
         for b in range(2):
-            cp(V("dh", DW * b + 1, DW * b + 1 + CAP), V("ps%d" % (4 + b), 0, CAP))
             act(V("dh", DW * (b + 2) + 1, DW * (b + 2) + 1 + CAP), V("ps%d" % (6 + b), 0, CAP))
-        for b in range(2):
-            tt(V(new, o + b, o + 4 * C, 4), V("dh", DW * b, DW * b + CAP + 2), V("fs", FW * b, FW * b + C), A.add, noff, G("tn"))
-            act(V("gg", C * b, C * b + C), V("dh", DW * (b + 2), DW * (b + 2) + CAP + 2), noff)
-        for b in range(2):
-            tt(V(new, o + 2 + b, o + 4 * C, 4), V("gg", C * b, C * b + C), V("ps%d" % (2 + b), 0, C), A.add, grp=G("tn"))
-        if t < NR - 1:
-            quant("qb", 0, 512, V("t1"))
-        else:
-            cp(V("back", 0, BLK), V("up", 32, 32 + BLK))
-            quant("qy", 0, C, V("t2"))
+            cp(V("dh", DW * b + 1, DW * b + 1 + CAP), V("ps%d" % (4 + b), 0, CAP))
+        for h, (a, b) in enumerate(LAST if final else RUNS):
+            noff = V("noff", a // 16, b // 16)
+            own, lent = ((0, 1), (2, 3)) if h == 0 else ((0,), (2, 3, 1))
+            for p in lent:
+                act(V("gg", C * (p - 1) + a, C * (p - 1) + b), V("dh", DW * p, DW * p + CAP + 2), noff)
+            for p in own:
+                tt(V(new, 4 * a + p, 4 * b, 4), V("dh", DW * p, DW * p + CAP + 2), V("fs", FW * p + a, FW * p + b), A.add,
+                   noff, G("new%d" % h))
+            for p in lent:
+                tt(V(new, 4 * a + p, 4 * b, 4), V("gg", C * (p - 1) + a, C * (p - 1) + b), V("ps%d" % p, a, b), A.add,
+                   grp=G("new%d" % h))
+            quant(qn, a, b, V(new, 4 * a, 4 * b))
+            mm(4 + h, "qv" if final else "qu", 0, qn, a, b)
+            if final:
+                stores.append(dma("y", T.oc[:, 4 * a:4 * b], bytes_of(V("qyc", a, b)), [V("qyc", a, b)], [], "out"))
 
-    for h, (a, b) in enumerate(((0, 256), (256, C))):
-        pick("qz", "qy", V("back", a // 16, b // 16), a, b)
-        mm(4 + h, "qv", 0, "qz", a, b)
-        stores.append(dma("y", T.oc[:, 4 * a:4 * b], bytes_of(V("qzc", a, b)), [V("qzc", a, b)], [], "out"))
+    a = LAST[0][1]
+    act(V("ysb", 0, a), V("ps4", 0, a))
+    stores.append(dma("s", T.y[:, 0:a], T.ysb[:, 0:a], [V("ysb", 0, a)], [], "out"))
+    cp(V("ysb", a, C), V("ps5", 0, C - a))
     for k in range(4):
-        stores.append(dma("y", T.osc[4 * k:4 * k + 4, :], T.qzs[32 * k:32 * k + 4, :], [V("qzs")], [], "out"))
-    cp(V("ysb", 0, 256), V("ps4", 0, 256))
-    act(V("ysb", 256, C), V("ps5", 0, C - 256))
-    stores.append(dma("y", T.y[:, 0:256], T.ysb[:, 0:256], [V("ysb", 0, 256)], [], "out"))
-    stores.append(dma("s", T.y[:, 256:C], T.ysb[:, 256:C], [V("ysb", 256, C)], [], "out"))
+        stores.append(dma("ss sy"[k + k // 2], T.osc[4 * k:4 * k + 4, :], T.qys[32 * k:32 * k + 4, :], [V("qys")], [], "out"))
+    stores.append(dma("y", T.y[:, a:C], T.ysb[:, a:C], [V("ysb", a, C)], [], "out"))
     op("y", "end", None, [], [], after=stores)
     plan(g, T, ops)
     g.wait_ge(T.sem.sent, sent[0])

@@ -2,13 +2,15 @@ from concourse.mybir import dt, AluOpType as A, AxisListType, ActivationFunction
 
 C, CAP, NR = 480, 160, 2
 BLK = 32
-FW, DW = 496, 176
-SL = 2 * (CAP + 16)
+DW = 176
+SL = 2 * CAP + 2
 SPARE = 1100
-EWID = 2560
+EWID = 2400
 BIG = 4.5e29
-RUNS = ((0, 256), (256, C))
-LAST = ((0, 320), (320, C))
+FIRST = (0, 192, 352, C)
+RUNS = ((0, 224, 352, C), (0, 224, 352, C))
+OWN = ((2, 1, 1), (2, 1, 1))
+PV = 20
 
 F32, BF, I32, U16, X4, U8 = "float32", "bfloat16", "int32", "uint16", "float8_e4m3fn_x4", "uint8"
 SCRATCH = {}
@@ -24,18 +26,18 @@ for _n, _w in (("wl", 512), ("wr0", 512), ("wr1", 512), ("qu", 128), ("qv", 128)
     _sb(_n + "s", _w, U8)
 _sb("hand", 256, X4)
 for _n, _w in (("xt", 4 * C), ("ut", 512), ("vt", 512), ("zi", 520), ("et", 1056), ("t1", 4 * C), ("t2", 4 * C),
-               ("fs", 4 * FW), ("dh", 4 * DW), ("gg", 3 * C), ("pt0", 4 * CAP), ("pt1", 4 * CAP), ("ht0", 4 * CAP),
-               ("ht1", 4 * CAP), ("ge", 200), ("rl", 200), ("sg", 168), ("pat", 168), ("m2", 168)):
+               ("fs", 4 * C + 16), ("dh", 4 * DW), ("gg", 4 * C), ("pt0", 4 * CAP), ("pt1", 4 * CAP), ("ht0", 4 * CAP),
+               ("ht1", 4 * CAP), ("ge", 200), ("rl", 200), ("sg", 168), ("pat", 168), ("m2", 168), ("vals", 256),
+               ("er0", EWID), ("er1", EWID), ("zs", 160), ("dk", 328), ("ea", 320), ("eb", 320)):
     _sb(_n, _w, BF)
-for _n, _w in (("kr", 48), ("j16", 32), ("vals", 256), ("cf", 32), ("bl", 32), ("msk", 96), ("zz", 16), ("d0", 40),
-               ("er0", EWID), ("er1", EWID), ("alt", SL), ("es", SL), ("ta", 488), ("xg", 96), ("bb", 96),
-               ("dd", 40), ("nh", 40), ("u2", 40), ("hb", 16), ("hc", 16), ("sw", 16), ("xx", 32), ("apr", 16),
-               ("yy", 32), ("bs", 8), ("tb", 320), ("nw", 32), ("un", 32), ("x2", 32), ("y2", 32), ("mf", 32),
-               ("nf", 32), ("nb", 48), ("tn", 64), ("ysb", C)):
+for _n, _w in (("kr", 48), ("j16", 32), ("cf", 32), ("bl", 32), ("zz", 16), ("d0", 40), ("od", 72),
+               ("ta", 488), ("xg", 96), ("bb", 96), ("dd", 40), ("nh", 72), ("u2", 72), ("hb", 16), ("hc", 16),
+               ("sw", 16), ("apr", 16), ("yy", 32), ("yr", 32), ("bs", 8), ("nw", 64), ("un", 64), ("y2", 32),
+               ("mf", 32), ("nf", 32), ("nb", 48), ("tn", 64), ("ysb", C)):
     _sb(_n, _w, F32)
 _sb("pi", 8, I32)
 _sb("ci", 8, I32)
-for _n, _w in (("boff", 12), ("ew", 2), ("nof", 2), ("pos", 16), ("eoff", 16), ("noff", 32)):
+for _n, _w in (("boff", 12), ("nof", 2), ("pos", 16), ("eoff", 40), ("noff", 32)):
     _sb(_n, _w, U16)
 for _b in range(8):
     SCRATCH["ps%d" % _b] = ("psum", [128, 512], F32)
@@ -136,6 +138,10 @@ def send(g, T, topo, src, dst, out, in_, sem, mask):
     return g.remote_dma(out, in_, T.sem[sem], T.sem.sent, pid, rid, mask)
 
 
+def pairs(cuts):
+    return list(zip(cuts[:-1], cuts[1:]))
+
+
 def rank_program(g, core, T, topo):
     cores = list(T.cores)
     n = len(cores)
@@ -204,9 +210,6 @@ def rank_program(g, core, T, topo):
     def turn(out, in_, grp=None):
         return op("v", "turn " + out[1], lambda e: e.transpose(out[0], in_[0]), [in_], [out], grp)
 
-    def total(out, in_):
-        return op("v", "sum " + out[1], lambda e: e.tensor_reduce(out[0], in_[0], AxisListType.X, A.add), [in_], [out])
-
     def act(out, in_, off=None, scale=None, grp=None):
         if off is not None:
             return op("s", "acti " + out[1], lambda e: e.activation(out[0], in_[0].indirect(off[0]), AF.Copy),
@@ -218,6 +221,11 @@ def rank_program(g, core, T, topo):
     def line(out, in_, func, bias, scale, grp=None):
         return op("s", "line " + out[1], lambda e: e.activation(out[0], in_[0], func, bias=ap(bias), scale=scale),
                   [in_, bias], [out], grp)
+
+    def above(total, in_, scale):
+        junk = V("yr")
+        return op("s", "sum " + total[1],
+                  lambda e: e.activation(junk[0], in_[0], AF.Relu, scale=scale, accum_out=total[0]), [in_], [junk, total])
 
     def quant(q, a, b, in_, grp=None):
         c, s = V(q + "c", a, b), V(q + "s", a, b)
@@ -241,19 +249,24 @@ def rank_program(g, core, T, topo):
     def bytes_of(v):
         return v[0].bitcast(dt.uint8)
 
-    dma("s", T.xt[:, 0:1024], T.x[:, 0:1024], [], [V("xt", 0, 1024)])
+    def load_x(q, a, b):
+        dma(q, T.xt[:, 4 * a:4 * b], T.x[:, 4 * a:4 * b], [], [V("xt", 4 * a, 4 * b)])
+
+    load_x("s", FIRST[0], FIRST[1])
     dma("y", T.ut[:], T.u[:], [], [V("ut")])
-    dma("s", T.xt[:, 1024:1920], T.x[:, 1024:1920], [], [V("xt", 1024, 1920)])
-    dma("y", bytes_of(V("wlc", 256, 512)), T.wc[:, 1024:2048], [], [V("wlc", 256, 512)])
+    load_x("s", FIRST[1], FIRST[2])
+    load_x("y", FIRST[2], FIRST[3])
+    dma("s", bytes_of(V("wlc", 256, 512)), T.wc[:, 1024:2048], [], [V("wlc", 256, 512)])
     lw = dma("y", bytes_of(V("wlc", 0, 256)), T.wc[:, 0:1024], [], [V("wlc", 0, 256)])
     dma("s", T.wls[:], T.ws[:], [], [V("wls")])
     dma("y", T.vt[:], T.v[:], [], [V("vt")], after=[lw])
 
     iota(V("pi", 0, 1), [[0, 1]], 0, 1, True)
-    iota(V("zi"), [[1, 520]], -2, -4)
     iota(V("kr"), [[1, 48]], -1, 0)
     iota(V("j16"), [[16, 32]], 0, 0)
-    iota(V("vals"), [[2, 16], [BLK, 16]], 0, 0)
+    iota(V("zi"), [[1, 520]], -2, -4)
+    iota(V("zs"), [[0, 20], [1, 8]], 0, 0)
+    iota(V("vals"), [[8, 16], [128, 16]], -1024, 0)
     far = [cores[(rank - 1 - t) % n] for t in range(NR)]
     hp = helper_of(core, topo)
     out_mask = topo.mask(core, far[0])
@@ -276,156 +289,181 @@ def rank_program(g, core, T, topo):
     def col(k):
         return V("cf", k, k + 1)
 
-    ci, o16, par, low, p32 = col(0), col(1), col(4), col(5), col(6)
-    c32, o32 = col(8), col(9)
+    ci, o16, i4, par, low, p32, plane = col(0), col(1), col(3), col(4), col(5), col(6), col(7)
+    c32, pbeg, pend = col(8), col(9), col(13)
     pi = V("pi", 0, 1)
     fill(V("ge"), 0.0, "f0")
     fill(V("d0"), -1.0, "f0")
     fill(V("pat"), 1.0)
     fill(V("ta", C, C + 8), BIG, "f0")
     fill(V("nh", 0, 1), 1.0, "f0")
-    fill(V("fs", C, 4 * FW, FW), 0.0, "f0")
-    fill(V("alt", 0, SL, 2), 0.0, "f0")
-    fill(V("alt", 1, SL, 2), 1.0, "f0")
     ts(V("ci", 2, 3), pi, 4, A.arith_shift_right)
     ts(V("ci", 0, 1), pi, 15, A.bitwise_and, grp="i0")
     ts(V("ci", 1, 2), pi, 16, A.bitwise_and, grp="i0")
-    tt(V("ci", 3, 4), V("ci", 2, 3), pi, A.add)
+    ts(V("ci", 3, 4), pi, 2, A.arith_shift_right, 3, A.bitwise_and, grp="i0")
+    tt(V("pi", 1, 2), V("ci", 2, 3), pi, A.add)
     ts(V("ci", 5, 6), pi, 1, A.bitwise_and, grp="i0")
     ts(V("ci", 6, 7), pi, 31, A.bitwise_and, grp="i0")
-    ts(V("ci", 4, 5), V("ci", 3, 4), 1, A.bitwise_and, grp="i0")
+    ts(V("ci", 7, 8), pi, 3, A.bitwise_and, grp="i0")
+    ts(V("ci", 4, 5), V("pi", 1, 2), 1, A.bitwise_and, grp="i0")
     fill(V("pat", 0, 165, 5), 0.0)
-    cp(V("cf", 0, 7), V("ci", 0, 7))
-    fill(V("dh", 0, 4 * DW, DW), 0.0, "f1")
-    fill(V("dh", CAP + 1, 4 * DW, DW), 0.0, "f1")
-    for b in range(2):
-        ts(V("et", 528 * b, 528 * b + 520), V("zi"), float(b), A.is_equal)
+    fill(V("nh", 33, 65), 0.0, "f1")
+    fill(V("nw", 32, 64), 0.0, "f1")
+    cp(V("cf", 0, 8), V("ci", 0, 8))
+    fill(V("od", 0, 33), 1.0, "f1")
+    fill(V("fs", 4 * C, 4 * C + 4), 0.0, "f1")
+    fill(V("dk", 0, 1), 0.0, "f1")
     for t in range(NR):
-        line(V("er%d" % t, 0, SL), V("zi", 0, SL), AF.Identity, -100.0, 0.0)
+        line(V("er%d" % t, 0, SL), V("zi", 0, SL), AF.Identity, 4096.0, 0.0)
     ts(c32, ci, float(BLK), A.mult, grp="i1")
-    ts(o32, o16, 2.0, A.mult, grp="i1")
-    ts(col(10), ci, 16.0, A.mult, o16, A.add, grp="i1")
-    ts(col(11), par, 32.0, A.mult, o16, A.add, grp="i1")
-    ts(col(12), ci, low, A.subtract, 0.5, A.mult, grp="i1")
+    ts(V("od", 34, 65), V("kr", 1, 32), p32, A.is_equal, 1024.0, A.mult)
     ts(V("d0", 0, 4), V("d0", 0, 4), ci, A.mult, -1.0, A.max)
-    ts(V("msk", 32, 64), V("kr", 1, 33), p32, A.is_gt, grp="i4")
-    ts(V("msk", 64, 96), V("kr", 1, 33), o16, A.subtract, 15.0, A.is_le, grp="i4")
-    for b in range(4):
-        a = 528 * (b % 2) + 2 - 2 * (b // 2)
-        quant("qe", 128 * b, 128 * b + 128, V("et", a, a + 512), "qe")
+    fill(V("od", 33, 34), -1024.0, "i1")
     for t in range(NR):
         ts(V("bl", 6 * t, 6 * t + 6), V("j16", 0, 6), c32, A.add, float(t - BLK), A.add, grp="i2")
-    ts(col(13), low, 144.0, A.mult, col(10), A.add, grp="i2")
-    ts(V("bl", 16, 18), V("j16", 0, 2), 0.5, A.mult, col(11), A.add, grp="i2")
-    ts(V("zz"), V("kr", 1, 17), col(10), A.add, float(SPARE), A.add, grp="i2")
-    tt(V("msk", 0, 32), V("msk", 32, 64), V("msk", 64, 96), A.mult)
+    ts(V("od", 49, 50), p32, 15.0, A.is_lt, -1024.0, A.mult)
+    ts(col(10), ci, 16.0, A.mult, float(SPARE), A.add)
     ts(V("boff"), V("bl", 0, 12), 0.0, A.max, float(C), A.min)
+    for b in range(2):
+        ts(V("et", 528 * b, 528 * b + 520), V("zi"), float(b), A.is_equal)
+    ts(V("zz"), V("kr", 1, 17), col(10), A.add)
+
+    late = []
+    for b in range(4):
+        late.append(lambda b=b: quant("qe", 128 * b, 128 * b + 128,
+                                      V("et", 528 * (b % 2) + 2 - 2 * (b // 2), 528 * (b % 2) + 514 - 2 * (b // 2))))
+    late.append(lambda: (ts(V("sg", 0, 165, 5), V("kr", 2, 35), 2.0, A.mult),
+                         ts(pbeg, plane, 1024.0, A.add, grp="i3"), ts(pend, plane, float(4 * C), A.add, grp="i3")))
+    late.append(lambda: (ts(V("dk", 1, 320, 2), V("zs"), i4, A.is_equal, 8192.0, A.mult, grp="i4"),
+                         ts(V("dk", 2, 321, 2), V("zs"), i4, A.is_equal, 4.0, A.mult, grp="i4")))
+    late.append(lambda: (ts(col(11), par, 32.0, A.mult, o16, A.add, grp="i5"),
+                         ts(col(12), ci, low, A.subtract, 0.5, A.mult, grp="i5"),
+                         fill(V("dh", 0, 4 * DW, DW), 0.0, "f2")))
+    late.append(lambda: (ts(V("bl", 16, 18), V("j16", 0, 2), 0.5, A.mult, col(11), A.add),
+                         fill(V("dh", CAP + 1, 4 * DW, DW), 0.0, "f2")))
+    late.append(lambda: ts(V("nof"), V("bl", 16, 18), col(12), A.add))
+
+    def gap():
+        if late:
+            late.pop(0)()
 
     quant("qu", 0, 128, V("ut"))
-    for h, (a, b) in enumerate(RUNS):
+    runs = pairs(FIRST)
+    for h, (a, b) in enumerate(runs):
         quant("qa", a, b, V("xt", 4 * a, 4 * b))
         mm(4 + h, "qu", 0, "qa", a, b)
-        if h == 0:
-            ts(V("ew", 0, 1), col(13), 319.0, A.min)
-            ts(V("nof"), V("bl", 16, 18), col(12), A.add)
-            ts(V("sg", 0, 165, 5), V("kr", 2, 35), 2.0, A.mult)
+        if h != 1:
+            gap()
 
-    ones = V("pat", 1, 165, 5)
-    ones32 = V("pat", 1, 160, 5)
-    mask = V("msk", 0, 32)
     stores = []
     for t in range(NR):
         q, er, pt, ht, qp, qh = "q" + "ab"[t], "er%d" % t, "pt%d" % t, "ht%d" % t, "qp%d" % t, "qh%d" % t
         final = t == NR - 1
         G = lambda s: s + str(t)
+        for h, (a, b) in enumerate(runs):
+            turn(V("ta", a, b), V("ps%d" % (4 + h), 0, b - a), G("ta"))
+        gap()
+        cp(V("xg", 0, 64), V("ta", 0, C + 1), V("boff", 6 * t, 6 * t + 4))
+        act(V("xg", 64, 96), V("ta", 0, C + 1), V("boff", 6 * t + 4, 6 * t + 6))
+        gap()
         for b in range(4):
             mm(b, "qe", 128 * b, q, 0, C)
-        for b in range(4):
-            act(V("fs", FW * b, FW * b + C), V("ps%d" % b, 0, C))
-        for h, (a, b) in enumerate(RUNS):
-            turn(V("ta", a, b), V("ps%d" % (4 + h), 0, b - a), G("ta"))
-        cp(V("xg"), V("ta", 0, C + 1), V("boff", 6 * t, 6 * t + 6))
+        for b in range(3):
+            act(V("fs", b, 4 * C, 4), V("ps%d" % b, 0, C))
         turn(V("bb"), V("xg"))
+        gap()
         for k in range(1, 5):
             w = 40 - k
             tt(V("ge", 5 - k, 5 * w, 5), V("bb", 28 + k, 28 + k + w), V("bb", 28, 28 + w), A.is_ge, grp=G("ge"))
+        gap()
         scan(V("rl", 0, 195), V("ge", 0, 195), V("ge", 0, 195), 0.0, A.mult, A.add)
+        gap()
         scan(V("dd", 0, 39), V("d0", 0, 39), V("rl", 4, 195, 5), 4.0, A.add, A.max)
+        gap()
+        tt(V("nh", 1, 33), V("dd", 4, 36), V("dd", 3, 35), A.is_lt)
+        gap()
         for e in range(4):
             line(V("sg", 1 + e, 165, 5), V("dd", 3 + e, 36 + e), AF.Sign, 3.5 - e, -1.0, G("sg"))
-        tt(V("nh", 1, 33), V("dd", 4, 36), V("dd", 3, 35), A.is_lt)
-        scan(V("u2", 0, 33), ones, V("nh", 0, 33), 0.0, A.add, A.subtract)
+        scan(V("u2", 0, 65), V("od", 0, 65), V("nh", 0, 65), 0.0, A.add, A.subtract)
         tt(V("hb"), V("nh", 2, 33, 2), V("zz"), A.mult)
-        ts(V("xx"), mask, V("u2", 32, 33), A.mult, 2.0, A.mult)
+        turn(V("yy"), V("u2", 33, 65))
+        tt(V("sw"), V("u2", 1, 33, 2), V("u2", 2, 33, 2), A.add)
         tt(V("hc"), V("hb"), V("nh", 1, 33, 2), A.mult)
-        turn(V("yy"), V("xx"))
-        tt(V("sw"), V("u2", 0, 32, 2), V("u2", 1, 33, 2), A.add)
-        total(V("bs", 0, 1), V("yy"))
+        above(V("bs", 0, 1), V("yy"), 2.0)
+        act(V("fs", 3, 4 * C, 4), V("ps3", 0, C))
         tt(V("apr"), V("sw"), V("hc"), A.add)
-        ts(V("pos"), V("apr"), V("bs", 0, 1), A.add, o32, A.add)
+        scan(V("m2", 0, 165), V("pat", 0, 165), V("sg", 0, 165), 0.0, A.mult, A.add)
+        ts(V("pos"), V("apr"), V("bs", 0, 1), A.add)
+        tt(V("nw", 0, 32), V("m2", 9, 165, 5), V("m2", 4, 160, 5), A.is_equal)
         win, off, val = V(er), V("pos"), V("vals")
         op("v", "scatter", lambda e, win=win, off=off, val=val: e.tensor_copy(win[0].indirect(off[0]), val[0]), [off, val], [win])
-        scan(V("m2", 0, 165), V("pat", 0, 165), V("sg", 0, 165), 0.0, A.mult, A.add)
-        scan(V("es"), V("alt"), V(er, 0, SL), -200.0, A.add, A.max)
-        tt(V("nw"), V("m2", 9, 165, 5), V("m2", 4, 160, 5), A.not_equal)
-        turn(V("tb", 0, CAP), V("es", 1, 2 * CAP, 2), G("tb"))
-        turn(V("tb", CAP, 2 * CAP), V("es", 33, SL, 2), G("tb"))
-        scan(V("un"), ones32, V("nw"), 0.0, A.mult, A.add)
-        tsi(V("eoff"), V("tb"), V("ew", 0, 1), float(C), A.min)
-        ts(V("x2"), mask, V("un", BLK - 1, BLK), A.mult)
-        for b in range(2):
-            cp(V(pt, b, 4 * CAP, 4), V("fs", FW * b, FW * b + C + 1), V("eoff", 0, 10), G("pv"))
-            act(V(pt, b + 2, 4 * CAP, 4), V("fs", FW * (b + 2), FW * (b + 2) + C + 1), V("eoff", 0, 10), grp=G("pa"))
-        turn(V("y2"), V("x2"))
+        scan(V("un"), V("od", 1, 65), V("nw"), 0.0, A.add, A.subtract)
+        scan(V("ea", 0, 314), V("dk", 0, 314), V(er, 0, 314), 0.0, A.add, A.min)
+        scan(V("eb", 0, 314), V("dk", 0, 314), V(er, 8, SL), 0.0, A.add, A.min)
+        turn(V("y2"), V("un", 32, 64))
+        ts(V("eoff", 0, 40, 2), V("ea", 9, 314, 16), pbeg, A.add, pend, A.min, grp=G("eo"))
+        ts(V("eoff", 1, 40, 2), V("eb", 9, 314, 16), pbeg, A.add, pend, A.min, grp=G("eo"))
+        above(V("bs", 4, 5), V("y2"), 1.0)
+        cp(V(pt, 0, 16 * PV), V("fs", 0, 4 * C + 4), V("eoff", 0, PV))
+        act(V(pt, 16 * PV, 4 * CAP), V("fs", 0, 4 * C + 4), V("eoff", PV, 40))
+        ts(V("nb", 0, 32), V("un", 0, 32), V("bs", 4, 5), A.add, grp=G("nb"))
+        ts(V("nb", 32, 48), V("un", 0, 16), V("bs", 4, 5), A.add, grp=G("nb"))
         quant(qp, 0, CAP, V(pt))
         for b in (0, 2, 1, 3):
             mm(4 + b, "wr%d" % t, 128 * b, qp, 0, CAP)
-        total(V("bs", 4, 5), V("y2"))
-        ts(V("nb", 0, 32), V("un"), V("bs", 4, 5), A.add, grp=G("nb"))
-        ts(V("nb", 32, 48), V("un", 0, 16), V("bs", 4, 5), A.add, grp=G("nb"))
+        turn(V("tn", 0, 32), V("nb", 0, 32), G("tn"))
+        turn(V("tn", 32, 64), V("nb", 16, 48), G("tn"))
         if final:
             line(V("mf"), V("m2", 9, 165, 5), AF.Identity, c32, 0.5)
+            ts(V("nf"), V("nb", 0, 32), -1.0, A.add)
             for k in range(8):
                 stores.append(dma("y", T.ol[k:k + 1, 0:C], T.mf[16 * k:16 * k + 15, :], [V("mf")], [], "ol"))
+            for k in range(8):
+                stores.append(dma("y", T.ol[k:k + 1, C:2 * C], T.nf[16 * k:16 * k + 15, :], [V("nf")], [], "ol"))
         for b in range(2):
             ts(V(ht, b, 4 * CAP, 4), V("ps%d" % (4 + b), 0, CAP), 0.03125, A.mult, grp=G("hv"))
             act(V(ht, b + 2, 4 * CAP, 4), V("ps%d" % (6 + b), 0, CAP), scale=0.03125, grp=G("ha"))
-        turn(V("tn", 0, 32), V("nb", 0, 32), G("tn"))
-        turn(V("tn", 32, 64), V("nb", 16, 48), G("tn"))
+        tsi(V("noff"), V("tn"), V("nof"), float(CAP + 1), A.min)
         quant(qh, 0, CAP, V(ht))
         for b in (2, 0, 3, 1):
             mm(4 + b, "qe", 128 * b, qh, 0, CAP)
-        tsi(V("noff"), V("tn"), V("nof"), float(CAP + 1), A.min)
-        if final:
-            ts(V("nf"), V("nb", 0, 32), -1.0, A.add)
-            for k in range(8):
-                stores.append(dma("y", T.ol[k:k + 1, C:2 * C], T.nf[16 * k:16 * k + 15, :], [V("nf")], [], "ol"))
-        else:
+        if not final:
             quant("qv", 0, 128, V("vt"))
         new, qn = ("t2", "qy") if final else ("t1", "qb")
         for b in range(2):
             act(V("dh", DW * (b + 2) + 1, DW * (b + 2) + 1 + CAP), V("ps%d" % (6 + b), 0, CAP))
             cp(V("dh", DW * b + 1, DW * b + 1 + CAP), V("ps%d" % (4 + b), 0, CAP))
-        for h, (a, b) in enumerate(LAST if final else RUNS):
-            noff = V("noff", a // 16, b // 16)
-            own, lent = ((0, 1), (2, 3)) if h == 0 else ((0,), (2, 3, 1))
-            for p in lent:
-                act(V("gg", C * (p - 1) + a, C * (p - 1) + b), V("dh", DW * p, DW * p + CAP + 2), noff)
-            for p in own:
-                tt(V(new, 4 * a + p, 4 * b, 4), V("dh", DW * p, DW * p + CAP + 2), V("fs", FW * p + a, FW * p + b), A.add,
-                   noff, G("new%d" % h))
-            for p in lent:
-                tt(V(new, 4 * a + p, 4 * b, 4), V("gg", C * (p - 1) + a, C * (p - 1) + b), V("ps%d" % p, a, b), A.add,
-                   grp=G("new%d" % h))
+        runs = pairs(RUNS[t])
+
+        def finish(h, a, b):
             quant(qn, a, b, V(new, 4 * a, 4 * b))
             mm(4 + h, "qv" if final else "qu", 0, qn, a, b)
             if final:
                 stores.append(dma("y", T.oc[:, 4 * a:4 * b], bytes_of(V("qyc", a, b)), [V("qyc", a, b)], [], "out"))
 
-    a = LAST[0][1]
-    act(V("ysb", 0, a), V("ps4", 0, a))
-    stores.append(dma("s", T.y[:, 0:a], T.ysb[:, 0:a], [V("ysb", 0, a)], [], "out"))
-    cp(V("ysb", a, C), V("ps5", 0, C - a))
+        due = []
+        for h, (a, b) in enumerate(runs):
+            noff = V("noff", a // 16, b // 16)
+            own, lent = tuple(range(OWN[t][h])), tuple(p for p in (2, 3, 1, 0) if p >= OWN[t][h])
+            for p in lent:
+                act(V("gg", C * p + a, C * p + b), V("dh", DW * p, DW * p + CAP + 2), noff)
+            for p in own + lent:
+                if p in own:
+                    tt(V(new, 4 * a + p, 4 * b, 4), V("dh", DW * p, DW * p + CAP + 2), V("fs", 4 * a + p, 4 * b, 4), A.add,
+                       noff, G("new%d" % h))
+                else:
+                    tt(V(new, 4 * a + p, 4 * b, 4), V("gg", C * p + a, C * p + b), V("ps%d" % p, a, b), A.add,
+                       grp=G("new%d" % h))
+                if due:
+                    finish(*due.pop())
+            due.append((h, a, b))
+        finish(*due.pop())
+
+    for h, (a, b) in enumerate(runs[:-1]):
+        act(V("ysb", a, b), V("ps%d" % (4 + h), 0, b - a))
+        stores.append(dma("s", T.y[:, a:b], T.ysb[:, a:b], [V("ysb", a, b)], [], "out"))
+    a = runs[-1][0]
+    cp(V("ysb", a, C), V("ps%d" % (3 + len(runs)), 0, C - a))
     for k in range(4):
         stores.append(dma("ss sy"[k + k // 2], T.osc[4 * k:4 * k + 4, :], T.qys[32 * k:32 * k + 4, :], [V("qys")], [], "out"))
     stores.append(dma("y", T.y[:, a:C], T.ysb[:, a:C], [V("ysb", a, C)], [], "out"))

@@ -4,13 +4,23 @@ C, CAP, NR = 480, 160, 2
 BLK = 32
 DW = 176
 SL = 2 * CAP + 2
-SPARE = 1100
-EWID = 2400
+SPARE = (1100, 2200)
+EWID = 3300
 BIG = 4.5e29
+LOADS = (0, 352, C)
 FIRST = (0, 192, 352, C)
-RUNS = ((0, 224, 352, C), (0, 224, 352, C))
-OWN = ((2, 1, 1), (2, 1, 1))
-PV = 20
+RUNS = ((0, 192, 352, C), (0, 160, 320, C))
+NB = 160
+STEPS = ((("g", 2, 288, C), ("g", 1, NB, C), ("c", 1, 0, NB), ("c", 2, 0, NB), ("c", 0, 0, NB), ("c", 3, 0, NB),
+          ("o", 2, NB, 288), ("o", 0, NB, C), ("o", 3, NB, C), ("a", 1, NB, 320), ("a", 2, 288, 416), ("a", 1, 320, C),
+          ("q", 0), ("a", 2, 416, C), ("q", 1), ("q", 2)),
+         (("g", 2, 288, 352), ("c", 2, 0, NB), ("c", 3, 0, NB), ("c", 0, 0, NB), ("c", 1, 0, NB), ("g", 3, NB, C),
+          ("g", 2, 352, C), ("o", 0, NB, C), ("o", 1, NB, C), ("a", 2, 288, 352), ("q", 0), ("y", 0), ("o", 2, NB, 288),
+          ("a", 3, NB, 384), ("a", 3, 384, C), ("a", 2, 352, C), ("q", 1), ("q", 2), ("y", 1), ("y", 2)))
+STORES = (0, 160, C)
+PLANES = ((1, 2, 0, 3), (2, 3, 0, 1))
+VCOPY = ((2, 3), (0, 1))
+PS = 22
 
 F32, BF, I32, U16, X4, U8 = "float32", "bfloat16", "int32", "uint16", "float8_e4m3fn_x4", "uint8"
 SCRATCH = {}
@@ -21,24 +31,27 @@ def _sb(name, n, d):
 
 
 for _n, _w in (("wl", 512), ("wr0", 512), ("wr1", 512), ("qu", 128), ("qv", 128), ("qe", 512), ("qa", C),
-               ("qb", C), ("qy", C), ("qp0", CAP), ("qp1", CAP), ("qh0", CAP), ("qh1", CAP)):
+               ("qb", C), ("qy", C), ("qp0", CAP), ("qp1", CAP), ("qh0", CAP + 2), ("qh1", CAP + 2), ("qm", 1024),
+               ("pe0", NB), ("po0", NB), ("pe1", NB), ("po1", NB)):
     _sb(_n + "c", _w, X4)
     _sb(_n + "s", _w, U8)
 _sb("hand", 256, X4)
-for _n, _w in (("xt", 4 * C), ("ut", 512), ("vt", 512), ("zi", 520), ("et", 1056), ("t1", 4 * C), ("t2", 4 * C),
-               ("fs", 4 * C + 16), ("dh", 4 * DW), ("gg", 4 * C), ("pt0", 4 * CAP), ("pt1", 4 * CAP), ("ht0", 4 * CAP),
-               ("ht1", 4 * CAP), ("ge", 200), ("rl", 200), ("sg", 168), ("pat", 168), ("m2", 168), ("vals", 256),
-               ("er0", EWID), ("er1", EWID), ("zs", 160), ("dk", 328), ("ea", 320), ("eb", 320)):
+for _n, _w in (("xt", 4 * C), ("ut", 512), ("vt", 512), ("zi", 128), ("et", 520), ("t1", 4 * C), ("t2", 4 * C),
+               ("fs", 4 * C + 16), ("dh", 4 * DW), ("gg", 4 * C), ("pt0", 4 * CAP), ("pt1", 4 * CAP),
+               ("ht0", 4 * CAP + 8), ("ht1", 4 * CAP + 8), ("em", 1040), ("zm", 256), ("ge", 200), ("rl", 200),
+               ("sg", 168), ("pat", 168), ("m2", 168), ("vals", 256), ("er0", EWID), ("er1", EWID), ("zs", 160),
+               ("dk", 328), ("ea", 320), ("eb", 320)):
     _sb(_n, _w, BF)
-for _n, _w in (("kr", 48), ("j16", 32), ("cf", 32), ("bl", 32), ("zz", 16), ("d0", 40), ("od", 72),
-               ("ta", 488), ("xg", 96), ("bb", 96), ("dd", 40), ("nh", 72), ("u2", 72), ("hb", 16), ("hc", 16),
-               ("sw", 16), ("apr", 16), ("yy", 32), ("yr", 32), ("bs", 8), ("nw", 64), ("un", 64), ("y2", 32),
-               ("mf", 32), ("nf", 32), ("nb", 48), ("tn", 64), ("ysb", C)):
+for _n, _w in (("j16", 32), ("cf", 32), ("d0", 40), ("od", 64), ("ta", 488), ("xg", 96), ("bb", 96), ("dd", 40),
+               ("nh", 64), ("u2", 64), ("hb", 16), ("hc", 16), ("sw", 16), ("apr", 16), ("yy", 32), ("yr", 32),
+               ("bs", 8), ("nw", 64), ("un", 64), ("y2", 32), ("mf", 32), ("nf", 32), ("nb", 48), ("tn", 64),
+               ("ysb", C)):
     _sb(_n, _w, F32)
-_sb("pi", 8, I32)
-_sb("ci", 8, I32)
-for _n, _w in (("boff", 12), ("nof", 2), ("pos", 16), ("eoff", 40), ("noff", 32)):
+_sb("ci", 16, I32)
+for _n, _w in (("boff", 12), ("nof", 2), ("pos", 16), ("eoff", 40), ("noff", 32), ("nob", 4), ("ne0", 16), ("no0", 16),
+               ("ne1", 16), ("no1", 16)):
     _sb(_n, _w, U16)
+SCRATCH["park"] = ("dram", [8, 512], F32)
 for _b in range(8):
     SCRATCH["ps%d" % _b] = ("psum", [128, 512], F32)
 
@@ -46,34 +59,22 @@ NCS, NDS = 100, 24
 SEMAPHORES = ["w0", "w1", "hin", "sent"] + ["c%d" % _k for _k in range(NCS)] + ["d%d" % _k for _k in range(NDS)]
 
 
-def plan(g, T, ops):
-    queues = {"g": g, "v": g.vector, "s": g.scalar, "p": g.tensor, "y": g.sync}
+def study(ops):
     node_of, members = [], {}
     for k, o in enumerate(ops):
         key = o["grp"] if o["grp"] is not None else k
         node_of.append(key)
         members.setdefault(key, []).append(k)
-    know = {q: 0 for q in queues}
-    at_issue, waits, touched = [], [], {}
+    know = {q: 0 for q in "gvspy"}
+    at_issue, waits = [], []
     for k, o in enumerate(ops):
-        deps = set(o["after"])
-        for acc, writes in [(a, False) for a in o["r"]] + [(a, True) for a in o["w"]]:
-            for j, cols, wrote in touched.get(acc[1], []):
-                bank = acc[1].startswith("ps") and ops[j]["q"] != o["q"]
-                if bank or ((writes or wrote) and cols & acc[2]):
-                    deps.add(j)
-        for acc in o["r"]:
-            touched.setdefault(acc[1], []).append((k, acc[2], False))
-        for acc in o["w"]:
-            touched.setdefault(acc[1], []).append((k, acc[2], True))
-        deps.discard(k)
         q = o["q"]
         if q is None:
             at_issue.append(0)
             waits.append([])
             continue
         need = {}
-        for j in deps:
+        for j in o["deps"]:
             if not know[q] >> j & 1:
                 nd = node_of[j]
                 assert nd != node_of[k] and max(members[nd]) < k, (o["name"], ops[j]["name"])
@@ -88,6 +89,54 @@ def plan(g, T, ops):
             know[q] |= need[nd]
         at_issue.append(know[q])
         waits.append(keep)
+    return node_of, members, at_issue, waits
+
+
+def joinable(ops, members, at_issue, waits):
+    waiters = {}
+    for k, w in enumerate(waits):
+        for nd in w:
+            waiters.setdefault(nd, []).append(k)
+    for w in waits:
+        for a in w:
+            for b in w:
+                ma, mb = members[a], members[b]
+                if a == b or any(ops[m]["dma"] or ops[m]["q"] is None for m in ma + mb):
+                    continue
+                if max(ma + mb) > min(waiters[a] + waiters[b]):
+                    continue
+                behind = len(set(ops[m]["q"] for m in ma + mb)) == 1 and max(ma) < max(mb)
+                if all(at_issue[k] >> m & 1 for k in waiters[a] for m in mb) and (
+                        behind or all(at_issue[k] >> m & 1 for k in waiters[b] for m in ma)):
+                    return ma + mb
+    return None
+
+
+def plan(g, T, ops):
+    queues = {"g": g, "v": g.vector, "s": g.scalar, "p": g.tensor, "y": g.sync}
+    touched = {}
+    for k, o in enumerate(ops):
+        deps = set(o["after"])
+        for acc, writes in [(a, False) for a in o["r"]] + [(a, True) for a in o["w"]]:
+            for j, cols, wrote in touched.get(acc[1], []):
+                bank = acc[1].startswith("ps")
+                if bank and ops[j]["q"] == o["q"] and o["adds"]:
+                    continue
+                if (bank and ops[j]["q"] != o["q"]) or ((writes or wrote) and cols & acc[2]):
+                    deps.add(j)
+        for acc in o["r"]:
+            touched.setdefault(acc[1], []).append((k, acc[2], False))
+        for acc in o["w"]:
+            touched.setdefault(acc[1], []).append((k, acc[2], True))
+        deps.discard(k)
+        o["deps"] = deps
+    while True:
+        node_of, members, at_issue, waits = study(ops)
+        both = joinable(ops, members, at_issue, waits)
+        if both is None:
+            break
+        for m in both:
+            ops[m]["grp"] = "join%d" % min(both)
     waited = set(nd for w in waits for nd in w)
     pools = {False: [["c%d" % k, 0, 0] for k in range(NCS)], True: [["d%d" % k, 0, 0] for k in range(NDS)]}
     signal = {}
@@ -171,23 +220,21 @@ def rank_program(g, core, T, topo):
         last = a + (len(range(a, b, step)) - 1) * step + 1
         return (T[name][:, a:last:step] if step > 1 else T[name][:, a:b], name, cols)
 
-    def op(q, name, fn, r, w, grp=None, dma=False, after=(), sem=None):
+    def op(q, name, fn, r, w, grp=None, dma=False, after=(), sem=None, adds=False):
         ops.append({"q": q, "name": name, "fn": fn, "r": [x for x in r if isinstance(x, tuple)], "w": list(w),
-                    "grp": grp, "dma": dma, "after": list(after), "sem": sem})
+                    "grp": grp, "dma": dma, "after": list(after), "sem": sem, "adds": adds})
         return len(ops) - 1
 
     def ap(x):
         return x[0] if isinstance(x, tuple) else x
 
-    def ts(out, in0, s1, o0, s2=None, o1=None, grp=None):
+    def ts(out, in0, s1, o0, s2=None, o1=None, grp=None, off=None):
+        src = (lambda: in0[0]) if off is None else (lambda: in0[0].indirect(off[0]))
         if o1 is None:
-            return op("v", "ts " + out[1], lambda e: e.tensor_scalar(out[0], in0[0], ap(s1), None, o0), [in0, s1], [out], grp)
-        return op("v", "ts " + out[1], lambda e: e.tensor_scalar(out[0], in0[0], ap(s1), ap(s2), o0, o1),
-                  [in0, s1, s2], [out], grp)
-
-    def tsi(out, in0, off, s1, o0):
-        return op("v", "tsi " + out[1], lambda e: e.tensor_scalar(out[0], in0[0].indirect(off[0]), s1, None, o0),
-                  [in0, off], [out])
+            return op("v", "ts " + out[1], lambda e: e.tensor_scalar(out[0], src(), ap(s1), None, o0),
+                      [in0, s1, off], [out], grp)
+        return op("v", "ts " + out[1], lambda e: e.tensor_scalar(out[0], src(), ap(s1), ap(s2), o0, o1),
+                  [in0, s1, s2, off], [out], grp)
 
     def tt(out, in0, in1, o, off=None, grp=None):
         if off is None:
@@ -219,8 +266,8 @@ def rank_program(g, core, T, topo):
         return op("s", "act " + out[1], lambda e: e.activation(out[0], in_[0], AF.Copy), [in_], [out], grp)
 
     def line(out, in_, func, bias, scale, grp=None):
-        return op("s", "line " + out[1], lambda e: e.activation(out[0], in_[0], func, bias=ap(bias), scale=scale),
-                  [in_, bias], [out], grp)
+        return op("s", "line " + out[1], lambda e: e.activation(out[0], in_[0], func, bias=ap(bias), scale=ap(scale)),
+                  [in_, bias, scale], [out], grp)
 
     def above(total, in_, scale):
         junk = V("yr")
@@ -231,17 +278,23 @@ def rank_program(g, core, T, topo):
         c, s = V(q + "c", a, b), V(q + "s", a, b)
         return op("v", "quant " + q, lambda e: e.quantize_mx(c[0], s[0], in_[0]), [in_], [c, s], grp)
 
-    def mm(bank, w, wa, x, a, b):
+    def mm(bank, w, wa, x, a, b, start=True, stop=True):
         out, wc, ws = V("ps%d" % bank, 0, b - a), V(w + "c", wa, wa + 128), V(w + "s", wa, wa + 128)
         xc, xs = V(x + "c", a, b), V(x + "s", a, b)
-        return op("p", "mm " + w + x, lambda e: e.matmul_mx(out[0], wc[0], ws[0], xc[0], xs[0], True, True),
-                  [wc, ws, xc, xs], [out])
+        return op("p", "mm " + w + x, lambda e: e.matmul_mx(out[0], wc[0], ws[0], xc[0], xs[0], start, stop),
+                  [wc, ws, xc, xs], [out], adds=not start)
 
-    def iota(out, pattern, base, cm, exact=False):
+    def pick(to, q, off):
+        c, s, qc, qs = V(to + "c"), V(to + "s"), V(q + "c"), V(q + "s")
+        op("v", "pick " + to, lambda e: e.tensor_copy(c[0].bitcast(dt.uint32), qc[0].bitcast(dt.uint32).indirect(off[0])),
+           [qc, off], [c])
+        act(s, qs, off)
+
+    def iota(out, pattern, base, cm, exact=False, grp=None):
         if exact:
-            return op("g", "iota " + out[1], lambda e: e.iota(out[0], pattern, base, cm), [], [out])
+            return op("g", "iota " + out[1], lambda e: e.iota(out[0], pattern, base, cm), [], [out], grp)
         return op("g", "iota " + out[1],
-                  lambda e: e.iota(out[0], pattern, base, cm, allow_small_or_imprecise_dtypes=True), [], [out])
+                  lambda e: e.iota(out[0], pattern, base, cm, allow_small_or_imprecise_dtypes=True), [], [out], grp)
 
     def dma(q, out, in_, r, w, grp=None, after=()):
         return op(q, "dma", lambda e: e.dma_start(out, in_), r, w, grp, True, after)
@@ -249,24 +302,24 @@ def rank_program(g, core, T, topo):
     def bytes_of(v):
         return v[0].bitcast(dt.uint8)
 
-    def load_x(q, a, b):
-        dma(q, T.xt[:, 4 * a:4 * b], T.x[:, 4 * a:4 * b], [], [V("xt", 4 * a, 4 * b)])
-
-    load_x("s", FIRST[0], FIRST[1])
-    dma("y", T.ut[:], T.u[:], [], [V("ut")])
-    load_x("s", FIRST[1], FIRST[2])
-    load_x("y", FIRST[2], FIRST[3])
+    lu = dma("s", T.ut[:], T.u[:], [], [V("ut")])
+    for a, b in pairs(LOADS):
+        dma("s", T.xt[:, 4 * a:4 * b], T.x[:, 4 * a:4 * b], [], [V("xt", 4 * a, 4 * b)])
     dma("s", bytes_of(V("wlc", 256, 512)), T.wc[:, 1024:2048], [], [V("wlc", 256, 512)])
-    lw = dma("y", bytes_of(V("wlc", 0, 256)), T.wc[:, 0:1024], [], [V("wlc", 0, 256)])
     dma("s", T.wls[:], T.ws[:], [], [V("wls")])
+    lw = dma("y", bytes_of(V("wlc", 0, 256)), T.wc[:, 0:1024], [], [V("wlc", 0, 256)], after=[lu])
     dma("y", T.vt[:], T.v[:], [], [V("vt")], after=[lw])
 
-    iota(V("pi", 0, 1), [[0, 1]], 0, 1, True)
-    iota(V("kr"), [[1, 48]], -1, 0)
+    iota(V("zi"), [[1, 128]], 0, -1)
+    iota(V("ci", 0, 12), [[1, NR], [16, 6]], 512 - BLK, BLK, True, "ci")
+    for k, cm in enumerate((32, 16, 128, 256)):
+        iota(V("ci", 12 + k, 13 + k), [[0, 1]], 0, cm, True, "ci")
     iota(V("j16"), [[16, 32]], 0, 0)
-    iota(V("zi"), [[1, 520]], -2, -4)
-    iota(V("zs"), [[0, 20], [1, 8]], 0, 0)
+    iota(V("zs"), [[0, 20], [128, 8]], 0, 0)
+    iota(V("zm", 0, 128), [[32, 4], [1016, 2], [1, 16]], 0, -1)
+    iota(V("zm", 128, 256), [[32, 4], [-984, 2], [1, 16]], 1000, -1)
     iota(V("vals"), [[8, 16], [128, 16]], -1024, 0)
+    iota(V("sg", 0, 165, 5), [[2, 33]], 2, 0)
     far = [cores[(rank - 1 - t) % n] for t in range(NR)]
     hp = helper_of(core, topo)
     out_mask = topo.mask(core, far[0])
@@ -280,8 +333,8 @@ def rank_program(g, core, T, topo):
     remote(hp, T.hand[:, 0:256].bitcast(dt.uint8), bytes_of(V("wlc", 256, 512)), V("wlc", 256, 512), "hin", on_mask)
     for t in range(NR):
         m = topo.mask(core, far[t])
-        remote(far[t], T["wr%dc" % t][:, 0:256].bitcast(dt.uint8), bytes_of(V("wlc", 0, 256)), V("wlc", 0, 256), "w%d" % t, m)
         remote(far[t], T["wr%ds" % t][:], T.wls[:], V("wls"), "w%d" % t, m)
+        remote(far[t], T["wr%dc" % t][:, 0:256].bitcast(dt.uint8), bytes_of(V("wlc", 0, 256)), V("wlc", 0, 256), "w%d" % t, m)
         giver = cores[(rank + 1 + t) % n]
         arrivals = 2 * count(topo.mask(giver, core)) + count(topo.mask(helper_of(giver, topo), core))
         op(None, "arrive", None, [], [V("wr%dc" % t), V("wr%ds" % t)], sem=("w%d" % t, arrivals))
@@ -289,71 +342,80 @@ def rank_program(g, core, T, topo):
     def col(k):
         return V("cf", k, k + 1)
 
-    ci, o16, i4, par, low, p32, plane = col(0), col(1), col(3), col(4), col(5), col(6), col(7)
-    c32, pbeg, pend = col(8), col(9), col(13)
-    pi = V("pi", 0, 1)
-    fill(V("ge"), 0.0, "f0")
-    fill(V("d0"), -1.0, "f0")
-    fill(V("pat"), 1.0)
-    fill(V("ta", C, C + 8), BIG, "f0")
-    fill(V("nh", 0, 1), 1.0, "f0")
-    ts(V("ci", 2, 3), pi, 4, A.arith_shift_right)
-    ts(V("ci", 0, 1), pi, 15, A.bitwise_and, grp="i0")
-    ts(V("ci", 1, 2), pi, 16, A.bitwise_and, grp="i0")
-    ts(V("ci", 3, 4), pi, 2, A.arith_shift_right, 3, A.bitwise_and, grp="i0")
-    tt(V("pi", 1, 2), V("ci", 2, 3), pi, A.add)
-    ts(V("ci", 5, 6), pi, 1, A.bitwise_and, grp="i0")
-    ts(V("ci", 6, 7), pi, 31, A.bitwise_and, grp="i0")
-    ts(V("ci", 7, 8), pi, 3, A.bitwise_and, grp="i0")
-    ts(V("ci", 4, 5), V("pi", 1, 2), 1, A.bitwise_and, grp="i0")
-    fill(V("pat", 0, 165, 5), 0.0)
-    fill(V("nh", 33, 65), 0.0, "f1")
-    fill(V("nw", 32, 64), 0.0, "f1")
-    cp(V("cf", 0, 8), V("ci", 0, 8))
-    fill(V("od", 0, 33), 1.0, "f1")
-    fill(V("fs", 4 * C, 4 * C + 4), 0.0, "f1")
-    fill(V("dk", 0, 1), 0.0, "f1")
-    for t in range(NR):
-        line(V("er%d" % t, 0, SL), V("zi", 0, SL), AF.Identity, 4096.0, 0.0)
-    ts(c32, ci, float(BLK), A.mult, grp="i1")
-    ts(V("od", 34, 65), V("kr", 1, 32), p32, A.is_equal, 1024.0, A.mult)
-    ts(V("d0", 0, 4), V("d0", 0, 4), ci, A.mult, -1.0, A.max)
-    fill(V("od", 33, 34), -1024.0, "i1")
-    for t in range(NR):
-        ts(V("bl", 6 * t, 6 * t + 6), V("j16", 0, 6), c32, A.add, float(t - BLK), A.add, grp="i2")
-    ts(V("od", 49, 50), p32, 15.0, A.is_lt, -1024.0, A.mult)
-    ts(col(10), ci, 16.0, A.mult, float(SPARE), A.add)
-    ts(V("boff"), V("bl", 0, 12), 0.0, A.max, float(C), A.min)
-    for b in range(2):
-        ts(V("et", 528 * b, 528 * b + 520), V("zi"), float(b), A.is_equal)
-    ts(V("zz"), V("kr", 1, 17), col(10), A.add)
+    def unit(b):
+        quant("qe", 128 * b, 128 * b + 128, V("et", 3 - b, 515 - b))
 
-    late = []
-    for b in range(4):
-        late.append(lambda b=b: quant("qe", 128 * b, 128 * b + 128,
-                                      V("et", 528 * (b % 2) + 2 - 2 * (b // 2), 528 * (b % 2) + 514 - 2 * (b // 2))))
-    late.append(lambda: (ts(V("sg", 0, 165, 5), V("kr", 2, 35), 2.0, A.mult),
-                         ts(pbeg, plane, 1024.0, A.add, grp="i3"), ts(pend, plane, float(4 * C), A.add, grp="i3")))
-    late.append(lambda: (ts(V("dk", 1, 320, 2), V("zs"), i4, A.is_equal, 8192.0, A.mult, grp="i4"),
-                         ts(V("dk", 2, 321, 2), V("zs"), i4, A.is_equal, 4.0, A.mult, grp="i4")))
-    late.append(lambda: (ts(col(11), par, 32.0, A.mult, o16, A.add, grp="i5"),
-                         ts(col(12), ci, low, A.subtract, 0.5, A.mult, grp="i5"),
-                         fill(V("dh", 0, 4 * DW, DW), 0.0, "f2")))
-    late.append(lambda: (ts(V("bl", 16, 18), V("j16", 0, 2), 0.5, A.mult, col(11), A.add),
-                         fill(V("dh", CAP + 1, 4 * DW, DW), 0.0, "f2")))
-    late.append(lambda: ts(V("nof"), V("bl", 16, 18), col(12), A.add))
+    def lay(out, c):
+        line(out, V("ge", 0, count(out[2])), AF.Identity, c, 0.0)
+
+    def half(k):
+        ts(V("em", 520 * k + 3, 520 * k + 515, 4), V("zm", 128 * k, 128 * k + 128), 0.0, A.is_equal)
+
+    def part(k):
+        a = 520 * (k // 4) + 3 - k % 4
+        quant("qm", 128 * k, 128 * k + 128, V("em", a, a + 512))
+
+    c32, p16, b128, low = col(12), col(13), col(14), col(15)
+    i4, pbeg, pend = col(16), col(17), col(18)
+    fill(V("ge"), 0.0)
+    fill(V("et"), 0.0)
+    fill(V("em", 0, 520), 0.0)
+    ts(V("et", 3, 515, 4), V("zi"), 0.0, A.is_equal)
+    lay(V("d0"), -1.0)
+    lay(V("od", 0, 32), 1.0)
+    lay(V("od", 32, 33), -1024.0)
+    lay(V("nh", 32, 64), 0.0)
+    lay(V("ta", C, C + 8), BIG)
+    lay(V("pat"), 1.0)
+    lay(V("er0", 0, 200), 4096.0)
+    lay(V("er0", 200, SL), 4096.0)
+    lay(V("pat", 0, 165, 5), 0.0)
+    lay(V("nw", 32, 64), 0.0)
+    lay(V("dk", 0, 1), 0.0)
+    lay(V("fs", 4 * C, 4 * C + 4), 0.0)
+    lay(V("dh", 0, 4 * DW, DW), 0.0)
+    lay(V("dh", CAP + 1, 4 * DW, DW), 0.0)
+    for t in range(NR):
+        lay(V("ht%d" % t, 4 * CAP, 4 * CAP + 8), 0.0)
+    unit(0)
+    unit(1)
+    ts(V("ci"), V("ci"), 511, A.bitwise_and)
+    unit(2)
+    cp(V("cf", 0, 16), V("ci"))
+    unit(3)
+    ts(V("boff"), V("cf", 0, 12), float(C), A.min)
+    quant("qu", 0, 128, V("ut"))
+    line(V("d0", 0, 4), V("d0", 0, 4), AF.Sign, 0.0, c32)
+    line(i4, b128, AF.Identity, c32, -0.25)
+    line(col(19), p16, AF.Identity, c32, -2.0)
+    line(col(20), low, AF.Identity, c32, -0.125)
+    line(pbeg, b128, AF.Identity, 1024.0, 1.0 / 128)
+    line(pend, b128, AF.Identity, float(4 * C), 1.0 / 128)
+    line(col(22), low, AF.Abs, col(19), 2.0)
+    line(col(21), col(19), AF.Identity, col(20), -2.0)
+    line(col(23), col(22), AF.Identity, col(21), 4.0)
+    line(col(24), col(19), AF.Identity, col(23), 2.0)
+    act(V("em", 520, 1040), V("em", 0, 520))
+
+    late = [lambda: (ts(V("od", 33, 64), V("j16", 0, 31), p16, A.is_equal, 1024.0, A.mult),
+                     ts(V("dk", 1, 320, 2), V("zs"), i4, A.is_equal, 8192.0, A.mult)),
+            lambda: (ts(V("od", 48, 49), p16, 240.0, A.is_lt, -1024.0, A.mult),
+                     ts(V("dk", 2, 321, 2), V("zs"), i4, A.is_equal, 4.0, A.mult)),
+            lambda: (half(0), half(1))]
+    late += [lambda k=k: part(k) for k in range(7)]
+    late += [lambda: (ts(V("nob", 0, 1), col(24), 1.0 / 64, A.mult),
+                      ts(V("nob", 2, 3), col(24), 1.0 / 64, A.mult, 16.0, A.add)),
+             lambda: (ts(V("nof"), V("zs", 0, 8, 4), col(23), A.add, 1.0 / 64, A.mult), part(7)),
+             lambda: None, lambda: None, lambda: quant("qv", 0, 128, V("vt"))]
 
     def gap():
         if late:
             late.pop(0)()
 
-    quant("qu", 0, 128, V("ut"))
     runs = pairs(FIRST)
     for h, (a, b) in enumerate(runs):
         quant("qa", a, b, V("xt", 4 * a, 4 * b))
         mm(4 + h, "qu", 0, "qa", a, b)
-        if h != 1:
-            gap()
 
     stores = []
     for t in range(NR):
@@ -368,7 +430,7 @@ def rank_program(g, core, T, topo):
         gap()
         for b in range(4):
             mm(b, "qe", 128 * b, q, 0, C)
-        for b in range(3):
+        for b in range(2):
             act(V("fs", b, 4 * C, 4), V("ps%d" % b, 0, C))
         turn(V("bb"), V("xg"))
         gap()
@@ -380,93 +442,104 @@ def rank_program(g, core, T, topo):
         gap()
         scan(V("dd", 0, 39), V("d0", 0, 39), V("rl", 4, 195, 5), 4.0, A.add, A.max)
         gap()
-        tt(V("nh", 1, 33), V("dd", 4, 36), V("dd", 3, 35), A.is_lt)
+        tt(V("nh", 0, 32), V("dd", 4, 36), V("dd", 3, 35), A.is_lt)
+        tt(V("hb"), V("dd", 3, 35, 2), V("dd", 5, 36, 2), A.subtract)
         gap()
         for e in range(4):
             line(V("sg", 1 + e, 165, 5), V("dd", 3 + e, 36 + e), AF.Sign, 3.5 - e, -1.0, G("sg"))
-        scan(V("u2", 0, 65), V("od", 0, 65), V("nh", 0, 65), 0.0, A.add, A.subtract)
-        tt(V("hb"), V("nh", 2, 33, 2), V("zz"), A.mult)
-        turn(V("yy"), V("u2", 33, 65))
-        tt(V("sw"), V("u2", 1, 33, 2), V("u2", 2, 33, 2), A.add)
-        tt(V("hc"), V("hb"), V("nh", 1, 33, 2), A.mult)
+        scan(V("u2"), V("od"), V("nh"), 0.0, A.add, A.subtract)
+        for k in range(2):
+            ts(V("hc", k, 16, 2), V("hb", k, 16, 2), 2.0, A.is_equal, float(SPARE[k]), A.mult, grp=G("hc"))
+        turn(V("yy"), V("u2", 32, 64))
+        tt(V("sw"), V("u2", 0, 32, 2), V("u2", 1, 32, 2), A.add)
         above(V("bs", 0, 1), V("yy"), 2.0)
-        act(V("fs", 3, 4 * C, 4), V("ps3", 0, C))
-        tt(V("apr"), V("sw"), V("hc"), A.add)
+        if not final:
+            line(V("er1", 0, SL), V("et", 0, SL), AF.Identity, 4096.0, 0.0)
+        for b in range(2, 4):
+            act(V("fs", b, 4 * C, 4), V("ps%d" % b, 0, C))
+        for b in range(4):
+            mm(b, "qe", 128 * b, q, 0, NB, stop=False)
         scan(V("m2", 0, 165), V("pat", 0, 165), V("sg", 0, 165), 0.0, A.mult, A.add)
-        ts(V("pos"), V("apr"), V("bs", 0, 1), A.add)
+        tt(V("apr"), V("sw"), V("hc"), A.add)
         tt(V("nw", 0, 32), V("m2", 9, 165, 5), V("m2", 4, 160, 5), A.is_equal)
+        gap()
+        ts(V("pos"), V("apr"), V("bs", 0, 1), A.add)
+        scan(V("un"), V("od"), V("nw"), 0.0, A.add, A.subtract)
+        gap()
         win, off, val = V(er), V("pos"), V("vals")
         op("v", "scatter", lambda e, win=win, off=off, val=val: e.tensor_copy(win[0].indirect(off[0]), val[0]), [off, val], [win])
-        scan(V("un"), V("od", 1, 65), V("nw"), 0.0, A.add, A.subtract)
-        scan(V("ea", 0, 314), V("dk", 0, 314), V(er, 0, 314), 0.0, A.add, A.min)
-        scan(V("eb", 0, 314), V("dk", 0, 314), V(er, 8, SL), 0.0, A.add, A.min)
         turn(V("y2"), V("un", 32, 64))
-        ts(V("eoff", 0, 40, 2), V("ea", 9, 314, 16), pbeg, A.add, pend, A.min, grp=G("eo"))
-        ts(V("eoff", 1, 40, 2), V("eb", 9, 314, 16), pbeg, A.add, pend, A.min, grp=G("eo"))
+        gap()
+        for a, b in ((0, 8 * PS), (8 * PS, 2 * CAP)):
+            scan(V("ea", a, b - 6), V("dk", 0, b - a - 6), V(er, a, b - 6), 0.0, A.add, A.min)
+            scan(V("eb", a, b - 6), V("dk", 0, b - a - 6), V(er, a + 8, b + 2), 0.0, A.add, A.min)
+        if final:
+            line(V("mf"), V("m2", 9, 165, 5), AF.Identity, c32, 0.5)
         above(V("bs", 4, 5), V("y2"), 1.0)
-        cp(V(pt, 0, 16 * PV), V("fs", 0, 4 * C + 4), V("eoff", 0, PV))
-        act(V(pt, 16 * PV, 4 * CAP), V("fs", 0, 4 * C + 4), V("eoff", PV, 40))
-        ts(V("nb", 0, 32), V("un", 0, 32), V("bs", 4, 5), A.add, grp=G("nb"))
-        ts(V("nb", 32, 48), V("un", 0, 16), V("bs", 4, 5), A.add, grp=G("nb"))
+        for a, b in ((0, PS), (PS, 40)):
+            ts(V("eoff", a, b, 2), V("ea", 8 * a + 9, 8 * b - 6, 16), pbeg, A.add, pend, A.min)
+            ts(V("eoff", a + 1, b, 2), V("eb", 8 * a + 9, 8 * b - 6, 16), pbeg, A.add, pend, A.min)
+        act(V(pt, 0, 16 * PS), V("fs", 0, 4 * C + 4), V("eoff", 0, PS))
+        cp(V(pt, 16 * PS, 4 * CAP), V("fs", 0, 4 * C + 4), V("eoff", PS, 40))
+        line(V("nb", 0, 32), V("un", 0, 32), AF.Identity, V("bs", 4, 5), 1.0, G("nb"))
+        line(V("nb", 32, 48), V("un", 0, 16), AF.Identity, V("bs", 4, 5), 1.0, G("nb"))
+        gap()
         quant(qp, 0, CAP, V(pt))
         for b in (0, 2, 1, 3):
             mm(4 + b, "wr%d" % t, 128 * b, qp, 0, CAP)
+        gap()
         turn(V("tn", 0, 32), V("nb", 0, 32), G("tn"))
         turn(V("tn", 32, 64), V("nb", 16, 48), G("tn"))
         if final:
-            line(V("mf"), V("m2", 9, 165, 5), AF.Identity, c32, 0.5)
-            ts(V("nf"), V("nb", 0, 32), -1.0, A.add)
-            for k in range(8):
-                stores.append(dma("y", T.ol[k:k + 1, 0:C], T.mf[16 * k:16 * k + 15, :], [V("mf")], [], "ol"))
-            for k in range(8):
-                stores.append(dma("y", T.ol[k:k + 1, C:2 * C], T.nf[16 * k:16 * k + 15, :], [V("nf")], [], "ol"))
+            line(V("nf"), V("nb", 0, 32), AF.Identity, -1.0, 1.0)
+            wide = dma("y", T.ol[:, 0:512], T.mf[:], [V("mf")], [])
+            first = dma("y", T.park[:], T.nf[:], [V("nf")], [])
+            stores.append(dma("y", T.ol[:, C:2 * C], T.park[:, 0:C], [], [], after=[first, wide]))
         for b in range(2):
             ts(V(ht, b, 4 * CAP, 4), V("ps%d" % (4 + b), 0, CAP), 0.03125, A.mult, grp=G("hv"))
             act(V(ht, b + 2, 4 * CAP, 4), V("ps%d" % (6 + b), 0, CAP), scale=0.03125, grp=G("ha"))
-        tsi(V("noff"), V("tn"), V("nof"), float(CAP + 1), A.min)
-        quant(qh, 0, CAP, V(ht))
-        for b in (2, 0, 3, 1):
+        for k in range(2):
+            ts(V(G("n" + "eo"[k])), V("tn"), 1.0, A.subtract, float(CAP), A.min, off=V("nob", 2 * k, 2 * k + 1))
+        ts(V("noff"), V("tn"), float(CAP + 1), A.min, off=V("nof"))
+        quant(qh, 0, CAP + 2, V(ht))
+        for b in PLANES[t]:
             mm(4 + b, "qe", 128 * b, qh, 0, CAP)
-        if not final:
-            quant("qv", 0, 128, V("vt"))
+        for k in range(2):
+            pick(G("p" + "eo"[k]), qh, V(G("n" + "eo"[k]), 0, NB // 16))
+            for b in PLANES[t]:
+                mm(b, "qm", 512 * k + 128 * b, G("p" + "eo"[k]), 0, NB, False, k == 1)
+        for b in PLANES[t]:
+            (cp if b in VCOPY[t] else act)(V("dh", DW * b + 1, DW * b + 1 + CAP), V("ps%d" % (4 + b), 0, CAP))
         new, qn = ("t2", "qy") if final else ("t1", "qb")
-        for b in range(2):
-            act(V("dh", DW * (b + 2) + 1, DW * (b + 2) + 1 + CAP), V("ps%d" % (6 + b), 0, CAP))
-            cp(V("dh", DW * b + 1, DW * b + 1 + CAP), V("ps%d" % (4 + b), 0, CAP))
         runs = pairs(RUNS[t])
-
-        def finish(h, a, b):
-            quant(qn, a, b, V(new, 4 * a, 4 * b))
-            mm(4 + h, "qv" if final else "qu", 0, qn, a, b)
-            if final:
-                stores.append(dma("y", T.oc[:, 4 * a:4 * b], bytes_of(V("qyc", a, b)), [V("qyc", a, b)], [], "out"))
-
-        due = []
-        for h, (a, b) in enumerate(runs):
-            noff = V("noff", a // 16, b // 16)
-            own, lent = tuple(range(OWN[t][h])), tuple(p for p in (2, 3, 1, 0) if p >= OWN[t][h])
-            for p in lent:
-                act(V("gg", C * p + a, C * p + b), V("dh", DW * p, DW * p + CAP + 2), noff)
-            for p in own + lent:
-                if p in own:
-                    tt(V(new, 4 * a + p, 4 * b, 4), V("dh", DW * p, DW * p + CAP + 2), V("fs", 4 * a + p, 4 * b, 4), A.add,
-                       noff, G("new%d" % h))
+        for step in STEPS[t]:
+            if step[0] in "qy":
+                a, b = runs[step[1]]
+                if step[0] == "q":
+                    quant(qn, a, b, V(new, 4 * a, 4 * b))
+                    mm(4 + step[1], "qv" if final else "qu", 0, qn, a, b)
                 else:
-                    tt(V(new, 4 * a + p, 4 * b, 4), V("gg", C * p + a, C * p + b), V("ps%d" % p, a, b), A.add,
-                       grp=G("new%d" % h))
-                if due:
-                    finish(*due.pop())
-            due.append((h, a, b))
-        finish(*due.pop())
+                    (cp if b == C else act)(V("ysb", a, b), V("ps%d" % (4 + step[1]), 0, b - a))
+                if final and b in STORES:
+                    a = STORES[STORES.index(b) - 1]
+                    if step[0] == "q":
+                        stores.append(dma("y", T.oc[:, 4 * a:4 * b], bytes_of(V("qyc", a, b)), [V("qyc", a, b)], [], "out"))
+                    else:
+                        stores.append(dma("s", T.y[:, a:b], T.ysb[:, a:b], [V("ysb", a, b)], [], "out"))
+                continue
+            p, a, b = step[1:]
+            noff, win = V("noff", a // 16, b // 16), V("dh", DW * p, DW * p + CAP + 2)
+            if step[0] == "c":
+                act(V(new, 4 * a + p, 4 * b, 4), V("ps%d" % p, a, b))
+            elif step[0] == "g":
+                act(V("gg", C * p + a, C * p + b), win, noff)
+            elif step[0] == "o":
+                tt(V(new, 4 * a + p, 4 * b, 4), win, V("fs", 4 * a + p, 4 * b, 4), A.add, noff)
+            else:
+                tt(V(new, 4 * a + p, 4 * b, 4), V("gg", C * p + a, C * p + b), V("ps%d" % p, a, b), A.add)
 
-    for h, (a, b) in enumerate(runs[:-1]):
-        act(V("ysb", a, b), V("ps%d" % (4 + h), 0, b - a))
-        stores.append(dma("s", T.y[:, a:b], T.ysb[:, a:b], [V("ysb", a, b)], [], "out"))
-    a = runs[-1][0]
-    cp(V("ysb", a, C), V("ps%d" % (3 + len(runs)), 0, C - a))
     for k in range(4):
-        stores.append(dma("ss sy"[k + k // 2], T.osc[4 * k:4 * k + 4, :], T.qys[32 * k:32 * k + 4, :], [V("qys")], [], "out"))
-    stores.append(dma("y", T.y[:, a:C], T.ysb[:, a:C], [V("ysb", a, C)], [], "out"))
+        stores.append(dma("y", T.osc[4 * k:4 * k + 4, :], T.qys[32 * k:32 * k + 4, :], [V("qys")], [], "out"))
     op("y", "end", None, [], [], after=stores)
     plan(g, T, ops)
     g.wait_ge(T.sem.sent, sent[0])

from concourse.mybir import dt, AluOpType as A, AxisListType, ActivationFunctionType as AF

C, CAP, NR = 480, 160, 2
BLK = 32
DW = 176
SL = 2 * CAP + 2
SPARE = (1100, 2200)
EWID = 3300
BIG = 4.5e29
LOADS = (0, 352, C)
FIRST = (0, 192, 352, C)
RUNS = ((0, 192, 352, C), (0, 160, 320, C))
NB = 160
STEPS = ((("g", 2, 288, C), ("g", 1, NB, C), ("c", 1, 0, NB), ("c", 2, 0, NB), ("c", 0, 0, NB), ("c", 3, 0, NB),
          ("o", 2, NB, 288), ("o", 0, NB, C), ("o", 3, NB, C), ("a", 1, NB, 320), ("a", 2, 288, 416), ("a", 1, 320, C),
          ("q", 0), ("a", 2, 416, C), ("q", 1), ("q", 2)),
         (("g", 2, 288, 352), ("c", 2, 0, NB), ("c", 3, 0, NB), ("c", 0, 0, NB), ("c", 1, 0, NB), ("g", 3, NB, C),
          ("g", 2, 352, C), ("o", 0, NB, C), ("o", 1, NB, C), ("a", 2, 288, 352), ("q", 0), ("y", 0), ("o", 2, NB, 288),
          ("a", 3, NB, 384), ("a", 3, 384, C), ("a", 2, 352, C), ("q", 1), ("q", 2), ("y", 1), ("y", 2)))
STORES = (0, 160, C)
PLANES = ((1, 2, 0, 3), (2, 3, 0, 1))
VCOPY = ((2, 3), (0, 1))
PS = 22

F32, BF, I32, U16, X4, U8 = "float32", "bfloat16", "int32", "uint16", "float8_e4m3fn_x4", "uint8"
SCRATCH = {}


def _sb(name, n, d):
    SCRATCH[name] = ("sbuf", [128, n], d)


for _n, _w in (("wl", 512), ("wr0", 512), ("wr1", 512), ("qu", 128), ("qv", 128), ("qe", 512), ("qa", C),
               ("qb", C), ("qy", C), ("qp0", CAP), ("qp1", CAP), ("qh0", CAP + 2), ("qh1", CAP + 2), ("qm", 1024),
               ("pe0", NB), ("po0", NB), ("pe1", NB), ("po1", NB)):
    _sb(_n + "c", _w, X4)
    _sb(_n + "s", _w, U8)
_sb("hand", 256, X4)
for _n, _w in (("xt", 4 * C), ("ut", 512), ("vt", 512), ("zi", 128), ("et", 520), ("t1", 4 * C), ("t2", 4 * C),
               ("fs", 4 * C + 16), ("dh", 4 * DW), ("gg", 4 * C), ("pt0", 4 * CAP), ("pt1", 4 * CAP),
               ("ht0", 4 * CAP + 8), ("ht1", 4 * CAP + 8), ("em", 1040), ("zm", 256), ("ge", 200), ("rl", 200),
               ("sg", 168), ("pat", 168), ("m2", 168), ("vals", 256), ("er0", EWID), ("er1", EWID), ("zs", 160),
               ("dk", 328), ("ea", 320), ("eb", 320)):
    _sb(_n, _w, BF)
for _n, _w in (("j16", 32), ("cf", 32), ("d0", 40), ("od", 64), ("ta", 488), ("xg", 96), ("bb", 96), ("dd", 40),
               ("nh", 64), ("u2", 64), ("hb", 16), ("hc", 16), ("sw", 16), ("apr", 16), ("yy", 32), ("yr", 32),
               ("bs", 8), ("nw", 64), ("un", 64), ("y2", 32), ("mf", 32), ("nf", 32), ("nb", 48), ("tn", 64),
               ("ysb", C)):
    _sb(_n, _w, F32)
_sb("ci", 16, I32)
for _n, _w in (("boff", 12), ("nof", 2), ("pos", 16), ("eoff", 40), ("noff", 32), ("nob", 4), ("ne0", 16), ("no0", 16),
               ("ne1", 16), ("no1", 16)):
    _sb(_n, _w, U16)
SCRATCH["park"] = ("dram", [8, 512], F32)
for _b in range(8):
    SCRATCH["ps%d" % _b] = ("psum", [128, 512], F32)

NCS, NDS = 100, 24
SEMAPHORES = ["w0", "w1", "hin", "sent"] + ["c%d" % _k for _k in range(NCS)] + ["d%d" % _k for _k in range(NDS)]


def study(ops):
    node_of, members = [], {}
    for k, o in enumerate(ops):
        key = o["grp"] if o["grp"] is not None else k
        node_of.append(key)
        members.setdefault(key, []).append(k)
    know = {q: 0 for q in "gvspy"}
    at_issue, waits = [], []
    for k, o in enumerate(ops):
        q = o["q"]
        if q is None:
            at_issue.append(0)
            waits.append([])
            continue
        need = {}
        for j in o["deps"]:
            if not know[q] >> j & 1:
                nd = node_of[j]
                assert nd != node_of[k] and max(members[nd]) < k, (o["name"], ops[j]["name"])
                cl = 0
                for m in members[nd]:
                    cl |= at_issue[m] | 1 << m
                need[nd] = cl
        keep = [nd for nd in need
                if not any(n2 != nd and all(need[n2] >> m & 1 for m in members[nd]) for n2 in need)]
        keep.sort(key=lambda nd: max(members[nd]))
        for nd in keep:
            know[q] |= need[nd]
        at_issue.append(know[q])
        waits.append(keep)
    return node_of, members, at_issue, waits


def joinable(ops, members, at_issue, waits):
    waiters = {}
    for k, w in enumerate(waits):
        for nd in w:
            waiters.setdefault(nd, []).append(k)
    for w in waits:
        for a in w:
            for b in w:
                ma, mb = members[a], members[b]
                if a == b or any(ops[m]["dma"] or ops[m]["q"] is None for m in ma + mb):
                    continue
                if max(ma + mb) > min(waiters[a] + waiters[b]):
                    continue
                behind = len(set(ops[m]["q"] for m in ma + mb)) == 1 and max(ma) < max(mb)
                if all(at_issue[k] >> m & 1 for k in waiters[a] for m in mb) and (
                        behind or all(at_issue[k] >> m & 1 for k in waiters[b] for m in ma)):
                    return ma + mb
    return None


def plan(g, T, ops):
    queues = {"g": g, "v": g.vector, "s": g.scalar, "p": g.tensor, "y": g.sync}
    touched = {}
    for k, o in enumerate(ops):
        deps = set(o["after"])
        for acc, writes in [(a, False) for a in o["r"]] + [(a, True) for a in o["w"]]:
            for j, cols, wrote in touched.get(acc[1], []):
                bank = acc[1].startswith("ps")
                if bank and ops[j]["q"] == o["q"] and o["adds"]:
                    continue
                if (bank and ops[j]["q"] != o["q"]) or ((writes or wrote) and cols & acc[2]):
                    deps.add(j)
        for acc in o["r"]:
            touched.setdefault(acc[1], []).append((k, acc[2], False))
        for acc in o["w"]:
            touched.setdefault(acc[1], []).append((k, acc[2], True))
        deps.discard(k)
        o["deps"] = deps
    while True:
        node_of, members, at_issue, waits = study(ops)
        both = joinable(ops, members, at_issue, waits)
        if both is None:
            break
        for m in both:
            ops[m]["grp"] = "join%d" % min(both)
    waited = set(nd for w in waits for nd in w)
    pools = {False: [["c%d" % k, 0, 0] for k in range(NCS)], True: [["d%d" % k, 0, 0] for k in range(NDS)]}
    signal = {}
    for k, o in enumerate(ops):
        nd = node_of[k]
        if nd in signal or nd not in waited:
            continue
        if o["q"] is None:
            signal[nd] = o["sem"]
            continue
        pool = pools[o["dma"]]
        for s in pool:
            if all(s[2] & ~at_issue[m] == 0 for m in members[nd]):
                break
        else:
            assert False, "out of semaphores"
        pool.remove(s)
        pool.append(s)
        s[1] += (16 if o["dma"] else 1) * len(members[nd])
        for m in members[nd]:
            s[2] |= 1 << m
        signal[nd] = (s[0], s[1])
    for k, o in enumerate(ops):
        if o["q"] is None:
            continue
        e = queues[o["q"]]
        for nd in waits[k]:
            e.wait_ge(T.sem[signal[nd][0]], signal[nd][1])
        if o["fn"] is None:
            continue
        ins = o["fn"](e)
        if node_of[k] in signal:
            ins.then_inc(T.sem[signal[node_of[k]][0]], 16 if o["dma"] else 1)
        else:
            assert not o["dma"], o["name"]


def helper_of(core, topo):
    return [c for c in topo.cores_of(core) if topo.die(c) != topo.die(core)][0]


def count(mask):
    return bin(mask).count("1")


def send(g, T, topo, src, dst, out, in_, sem, mask):
    rid, pid = topo.addr(dst, src)
    return g.remote_dma(out, in_, T.sem[sem], T.sem.sent, pid, rid, mask)


def pairs(cuts):
    return list(zip(cuts[:-1], cuts[1:]))


def rank_program(g, core, T, topo):
    cores = list(T.cores)
    n = len(cores)
    rank = T.rank_of(core)
    if rank is None:
        for r, c in enumerate(cores):
            if helper_of(c, topo) == core:
                far = [cores[(r - 1 - t) % n] for t in range(NR)]
                g.wait_ge(T.sem.hin, count(topo.mask(c, core) & ~topo.mask(c, far[0])))
                total = 0
                for t in range(NR):
                    m = topo.mask(core, far[t])
                    send(g, T, topo, core, far[t], T["wr%dc" % t][:, 256:512].bitcast(dt.uint8),
                         T.hand[:, 0:256].bitcast(dt.uint8), "w%d" % t, m)
                    total += count(m)
                g.wait_ge(T.sem.sent, total)
        return

    ops = []

    def V(name, a=None, b=None, step=1):
        if a is None:
            a, b = 0, SCRATCH[name][1][1]
        cols = 0
        for c in range(a, b, step):
            cols |= 1 << c
        last = a + (len(range(a, b, step)) - 1) * step + 1
        return (T[name][:, a:last:step] if step > 1 else T[name][:, a:b], name, cols)

    def op(q, name, fn, r, w, grp=None, dma=False, after=(), sem=None, adds=False):
        ops.append({"q": q, "name": name, "fn": fn, "r": [x for x in r if isinstance(x, tuple)], "w": list(w),
                    "grp": grp, "dma": dma, "after": list(after), "sem": sem, "adds": adds})
        return len(ops) - 1

    def ap(x):
        return x[0] if isinstance(x, tuple) else x

    def ts(out, in0, s1, o0, s2=None, o1=None, grp=None, off=None):
        src = (lambda: in0[0]) if off is None else (lambda: in0[0].indirect(off[0]))
        if o1 is None:
            return op("v", "ts " + out[1], lambda e: e.tensor_scalar(out[0], src(), ap(s1), None, o0),
                      [in0, s1, off], [out], grp)
        return op("v", "ts " + out[1], lambda e: e.tensor_scalar(out[0], src(), ap(s1), ap(s2), o0, o1),
                  [in0, s1, s2, off], [out], grp)

    def tt(out, in0, in1, o, off=None, grp=None):
        if off is None:
            return op("v", "tt " + out[1], lambda e: e.tensor_tensor(out[0], in0[0], in1[0], o), [in0, in1], [out], grp)
        return op("v", "tti " + out[1], lambda e: e.tensor_tensor(out[0], in0[0].indirect(off[0]), in1[0], o),
                  [in0, in1, off], [out], grp)

    def cp(out, in_, off=None, grp=None):
        if off is None:
            return op("v", "cp " + out[1], lambda e: e.tensor_copy(out[0], in_[0]), [in_], [out], grp)
        return op("v", "cpi " + out[1], lambda e: e.tensor_copy(out[0], in_[0].indirect(off[0])), [in_, off], [out], grp)

    def fill(out, c, grp=None):
        return op("v", "fill " + out[1], lambda e: e.memset(out[0], c), [], [out], grp)

    def scan(out, d0, d1, init, o0, o1):
        return op("v", "scan " + out[1], lambda e: e.tensor_tensor_scan(out[0], d0[0], d1[0], ap(init), o0, o1),
                  [d0, d1, init], [out])

    def turn(out, in_, grp=None):
        return op("v", "turn " + out[1], lambda e: e.transpose(out[0], in_[0]), [in_], [out], grp)

    def act(out, in_, off=None, scale=None, grp=None):
        if off is not None:
            return op("s", "acti " + out[1], lambda e: e.activation(out[0], in_[0].indirect(off[0]), AF.Copy),
                      [in_, off], [out], grp)
        if scale is not None:
            return op("s", "acts " + out[1], lambda e: e.activation(out[0], in_[0], AF.Copy, scale=scale), [in_], [out], grp)
        return op("s", "act " + out[1], lambda e: e.activation(out[0], in_[0], AF.Copy), [in_], [out], grp)

    def line(out, in_, func, bias, scale, grp=None):
        return op("s", "line " + out[1], lambda e: e.activation(out[0], in_[0], func, bias=ap(bias), scale=ap(scale)),
                  [in_, bias, scale], [out], grp)

    def above(total, in_, scale):
        junk = V("yr")
        return op("s", "sum " + total[1],
                  lambda e: e.activation(junk[0], in_[0], AF.Relu, scale=scale, accum_out=total[0]), [in_], [junk, total])

    def quant(q, a, b, in_, grp=None):
        c, s = V(q + "c", a, b), V(q + "s", a, b)
        return op("v", "quant " + q, lambda e: e.quantize_mx(c[0], s[0], in_[0]), [in_], [c, s], grp)

    def mm(bank, w, wa, x, a, b, start=True, stop=True):
        out, wc, ws = V("ps%d" % bank, 0, b - a), V(w + "c", wa, wa + 128), V(w + "s", wa, wa + 128)
        xc, xs = V(x + "c", a, b), V(x + "s", a, b)
        return op("p", "mm " + w + x, lambda e: e.matmul_mx(out[0], wc[0], ws[0], xc[0], xs[0], start, stop),
                  [wc, ws, xc, xs], [out], adds=not start)

    def pick(to, q, off):
        c, s, qc, qs = V(to + "c"), V(to + "s"), V(q + "c"), V(q + "s")
        op("v", "pick " + to, lambda e: e.tensor_copy(c[0].bitcast(dt.uint32), qc[0].bitcast(dt.uint32).indirect(off[0])),
           [qc, off], [c])
        act(s, qs, off)

    def iota(out, pattern, base, cm, exact=False, grp=None):
        if exact:
            return op("g", "iota " + out[1], lambda e: e.iota(out[0], pattern, base, cm), [], [out], grp)
        return op("g", "iota " + out[1],
                  lambda e: e.iota(out[0], pattern, base, cm, allow_small_or_imprecise_dtypes=True), [], [out], grp)

    def dma(q, out, in_, r, w, grp=None, after=()):
        return op(q, "dma", lambda e: e.dma_start(out, in_), r, w, grp, True, after)

    def bytes_of(v):
        return v[0].bitcast(dt.uint8)

    lu = dma("s", T.ut[:], T.u[:], [], [V("ut")])
    for a, b in pairs(LOADS):
        dma("s", T.xt[:, 4 * a:4 * b], T.x[:, 4 * a:4 * b], [], [V("xt", 4 * a, 4 * b)])
    dma("s", bytes_of(V("wlc", 256, 512)), T.wc[:, 1024:2048], [], [V("wlc", 256, 512)])
    dma("s", T.wls[:], T.ws[:], [], [V("wls")])
    lw = dma("y", bytes_of(V("wlc", 0, 256)), T.wc[:, 0:1024], [], [V("wlc", 0, 256)], after=[lu])
    dma("y", T.vt[:], T.v[:], [], [V("vt")], after=[lw])

    iota(V("zi"), [[1, 128]], 0, -1)
    iota(V("ci", 0, 12), [[1, NR], [16, 6]], 512 - BLK, BLK, True, "ci")
    for k, cm in enumerate((32, 16, 128, 256)):
        iota(V("ci", 12 + k, 13 + k), [[0, 1]], 0, cm, True, "ci")
    iota(V("j16"), [[16, 32]], 0, 0)
    iota(V("zs"), [[0, 20], [128, 8]], 0, 0)
    iota(V("zm", 0, 128), [[32, 4], [1016, 2], [1, 16]], 0, -1)
    iota(V("zm", 128, 256), [[32, 4], [-984, 2], [1, 16]], 1000, -1)
    iota(V("vals"), [[8, 16], [128, 16]], -1024, 0)
    iota(V("sg", 0, 165, 5), [[2, 33]], 2, 0)
    far = [cores[(rank - 1 - t) % n] for t in range(NR)]
    hp = helper_of(core, topo)
    out_mask = topo.mask(core, far[0])
    on_mask = topo.mask(core, hp) & ~out_mask
    sent = [0]

    def remote(dst, out, in_, src, sem, mask):
        op("g", "remote", lambda e: send(e, T, topo, core, dst, out, in_, sem, mask), [src], [])
        sent[0] += count(mask)

    remote(hp, T.hand[:, 0:256].bitcast(dt.uint8), bytes_of(V("wlc", 256, 512)), V("wlc", 256, 512), "hin", on_mask)
    for t in range(NR):
        m = topo.mask(core, far[t])
        remote(far[t], T["wr%ds" % t][:], T.wls[:], V("wls"), "w%d" % t, m)
        remote(far[t], T["wr%dc" % t][:, 0:256].bitcast(dt.uint8), bytes_of(V("wlc", 0, 256)), V("wlc", 0, 256), "w%d" % t, m)
        giver = cores[(rank + 1 + t) % n]
        arrivals = 2 * count(topo.mask(giver, core)) + count(topo.mask(helper_of(giver, topo), core))
        op(None, "arrive", None, [], [V("wr%dc" % t), V("wr%ds" % t)], sem=("w%d" % t, arrivals))

    def col(k):
        return V("cf", k, k + 1)

    def unit(b):
        quant("qe", 128 * b, 128 * b + 128, V("et", 3 - b, 515 - b))

    def lay(out, c):
        line(out, V("ge", 0, count(out[2])), AF.Identity, c, 0.0)

    def half(k):
        ts(V("em", 520 * k + 3, 520 * k + 515, 4), V("zm", 128 * k, 128 * k + 128), 0.0, A.is_equal)

    def part(k):
        a = 520 * (k // 4) + 3 - k % 4
        quant("qm", 128 * k, 128 * k + 128, V("em", a, a + 512))

    c32, p16, b128, low = col(12), col(13), col(14), col(15)
    i4, pbeg, pend = col(16), col(17), col(18)
    fill(V("ge"), 0.0)
    fill(V("et"), 0.0)
    fill(V("em", 0, 520), 0.0)
    ts(V("et", 3, 515, 4), V("zi"), 0.0, A.is_equal)
    lay(V("d0"), -1.0)
    lay(V("od", 0, 32), 1.0)
    lay(V("od", 32, 33), -1024.0)
    lay(V("nh", 32, 64), 0.0)
    lay(V("ta", C, C + 8), BIG)
    lay(V("pat"), 1.0)
    lay(V("er0", 0, 200), 4096.0)
    lay(V("er0", 200, SL), 4096.0)
    lay(V("pat", 0, 165, 5), 0.0)
    lay(V("nw", 32, 64), 0.0)
    lay(V("dk", 0, 1), 0.0)
    lay(V("fs", 4 * C, 4 * C + 4), 0.0)
    lay(V("dh", 0, 4 * DW, DW), 0.0)
    lay(V("dh", CAP + 1, 4 * DW, DW), 0.0)
    for t in range(NR):
        lay(V("ht%d" % t, 4 * CAP, 4 * CAP + 8), 0.0)
    unit(0)
    unit(1)
    ts(V("ci"), V("ci"), 511, A.bitwise_and)
    unit(2)
    cp(V("cf", 0, 16), V("ci"))
    unit(3)
    ts(V("boff"), V("cf", 0, 12), float(C), A.min)
    quant("qu", 0, 128, V("ut"))
    line(V("d0", 0, 4), V("d0", 0, 4), AF.Sign, 0.0, c32)
    line(i4, b128, AF.Identity, c32, -0.25)
    line(col(19), p16, AF.Identity, c32, -2.0)
    line(col(20), low, AF.Identity, c32, -0.125)
    line(pbeg, b128, AF.Identity, 1024.0, 1.0 / 128)
    line(pend, b128, AF.Identity, float(4 * C), 1.0 / 128)
    line(col(22), low, AF.Abs, col(19), 2.0)
    line(col(21), col(19), AF.Identity, col(20), -2.0)
    line(col(23), col(22), AF.Identity, col(21), 4.0)
    line(col(24), col(19), AF.Identity, col(23), 2.0)
    act(V("em", 520, 1040), V("em", 0, 520))

    late = [lambda: (ts(V("od", 33, 64), V("j16", 0, 31), p16, A.is_equal, 1024.0, A.mult),
                     ts(V("dk", 1, 320, 2), V("zs"), i4, A.is_equal, 8192.0, A.mult)),
            lambda: (ts(V("od", 48, 49), p16, 240.0, A.is_lt, -1024.0, A.mult),
                     ts(V("dk", 2, 321, 2), V("zs"), i4, A.is_equal, 4.0, A.mult)),
            lambda: (half(0), half(1))]
    late += [lambda k=k: part(k) for k in range(7)]
    late += [lambda: (ts(V("nob", 0, 1), col(24), 1.0 / 64, A.mult),
                      ts(V("nob", 2, 3), col(24), 1.0 / 64, A.mult, 16.0, A.add)),
             lambda: (ts(V("nof"), V("zs", 0, 8, 4), col(23), A.add, 1.0 / 64, A.mult), part(7)),
             lambda: None, lambda: None, lambda: quant("qv", 0, 128, V("vt"))]

    def gap():
        if late:
            late.pop(0)()

    runs = pairs(FIRST)
    for h, (a, b) in enumerate(runs):
        quant("qa", a, b, V("xt", 4 * a, 4 * b))
        mm(4 + h, "qu", 0, "qa", a, b)

    stores = []
    for t in range(NR):
        q, er, pt, ht, qp, qh = "q" + "ab"[t], "er%d" % t, "pt%d" % t, "ht%d" % t, "qp%d" % t, "qh%d" % t
        final = t == NR - 1
        G = lambda s: s + str(t)
        for h, (a, b) in enumerate(runs):
            turn(V("ta", a, b), V("ps%d" % (4 + h), 0, b - a), G("ta"))
        gap()
        cp(V("xg", 0, 64), V("ta", 0, C + 1), V("boff", 6 * t, 6 * t + 4))
        act(V("xg", 64, 96), V("ta", 0, C + 1), V("boff", 6 * t + 4, 6 * t + 6))
        gap()
        for b in range(4):
            mm(b, "qe", 128 * b, q, 0, C)
        for b in range(2):
            act(V("fs", b, 4 * C, 4), V("ps%d" % b, 0, C))
        turn(V("bb"), V("xg"))
        gap()
        for k in range(1, 5):
            w = 40 - k
            tt(V("ge", 5 - k, 5 * w, 5), V("bb", 28 + k, 28 + k + w), V("bb", 28, 28 + w), A.is_ge, grp=G("ge"))
        gap()
        scan(V("rl", 0, 195), V("ge", 0, 195), V("ge", 0, 195), 0.0, A.mult, A.add)
        gap()
        scan(V("dd", 0, 39), V("d0", 0, 39), V("rl", 4, 195, 5), 4.0, A.add, A.max)
        gap()
        tt(V("nh", 0, 32), V("dd", 4, 36), V("dd", 3, 35), A.is_lt)
        tt(V("hb"), V("dd", 3, 35, 2), V("dd", 5, 36, 2), A.subtract)
        gap()
        for e in range(4):
            line(V("sg", 1 + e, 165, 5), V("dd", 3 + e, 36 + e), AF.Sign, 3.5 - e, -1.0, G("sg"))
        scan(V("u2"), V("od"), V("nh"), 0.0, A.add, A.subtract)
        for k in range(2):
            ts(V("hc", k, 16, 2), V("hb", k, 16, 2), 2.0, A.is_equal, float(SPARE[k]), A.mult, grp=G("hc"))
        turn(V("yy"), V("u2", 32, 64))
        tt(V("sw"), V("u2", 0, 32, 2), V("u2", 1, 32, 2), A.add)
        above(V("bs", 0, 1), V("yy"), 2.0)
        if not final:
            line(V("er1", 0, SL), V("et", 0, SL), AF.Identity, 4096.0, 0.0)
        for b in range(2, 4):
            act(V("fs", b, 4 * C, 4), V("ps%d" % b, 0, C))
        for b in range(4):
            mm(b, "qe", 128 * b, q, 0, NB, stop=False)
        scan(V("m2", 0, 165), V("pat", 0, 165), V("sg", 0, 165), 0.0, A.mult, A.add)
        tt(V("apr"), V("sw"), V("hc"), A.add)
        tt(V("nw", 0, 32), V("m2", 9, 165, 5), V("m2", 4, 160, 5), A.is_equal)
        gap()
        ts(V("pos"), V("apr"), V("bs", 0, 1), A.add)
        scan(V("un"), V("od"), V("nw"), 0.0, A.add, A.subtract)
        gap()
        win, off, val = V(er), V("pos"), V("vals")
        op("v", "scatter", lambda e, win=win, off=off, val=val: e.tensor_copy(win[0].indirect(off[0]), val[0]), [off, val], [win])
        turn(V("y2"), V("un", 32, 64))
        gap()
        for a, b in ((0, 8 * PS), (8 * PS, 2 * CAP)):
            scan(V("ea", a, b - 6), V("dk", 0, b - a - 6), V(er, a, b - 6), 0.0, A.add, A.min)
            scan(V("eb", a, b - 6), V("dk", 0, b - a - 6), V(er, a + 8, b + 2), 0.0, A.add, A.min)
        if final:
            line(V("mf"), V("m2", 9, 165, 5), AF.Identity, c32, 0.5)
        above(V("bs", 4, 5), V("y2"), 1.0)
        for a, b in ((0, PS), (PS, 40)):
            ts(V("eoff", a, b, 2), V("ea", 8 * a + 9, 8 * b - 6, 16), pbeg, A.add, pend, A.min)
            ts(V("eoff", a + 1, b, 2), V("eb", 8 * a + 9, 8 * b - 6, 16), pbeg, A.add, pend, A.min)
        act(V(pt, 0, 16 * PS), V("fs", 0, 4 * C + 4), V("eoff", 0, PS))
        cp(V(pt, 16 * PS, 4 * CAP), V("fs", 0, 4 * C + 4), V("eoff", PS, 40))
        line(V("nb", 0, 32), V("un", 0, 32), AF.Identity, V("bs", 4, 5), 1.0, G("nb"))
        line(V("nb", 32, 48), V("un", 0, 16), AF.Identity, V("bs", 4, 5), 1.0, G("nb"))
        gap()
        quant(qp, 0, CAP, V(pt))
        for b in (0, 2, 1, 3):
            mm(4 + b, "wr%d" % t, 128 * b, qp, 0, CAP)
        gap()
        turn(V("tn", 0, 32), V("nb", 0, 32), G("tn"))
        turn(V("tn", 32, 64), V("nb", 16, 48), G("tn"))
        if final:
            line(V("nf"), V("nb", 0, 32), AF.Identity, -1.0, 1.0)
            wide = dma("y", T.ol[:, 0:512], T.mf[:], [V("mf")], [])
            first = dma("y", T.park[:], T.nf[:], [V("nf")], [])
            stores.append(dma("y", T.ol[:, C:2 * C], T.park[:, 0:C], [], [], after=[first, wide]))
        for b in range(2):
            ts(V(ht, b, 4 * CAP, 4), V("ps%d" % (4 + b), 0, CAP), 0.03125, A.mult, grp=G("hv"))
            act(V(ht, b + 2, 4 * CAP, 4), V("ps%d" % (6 + b), 0, CAP), scale=0.03125, grp=G("ha"))
        for k in range(2):
            ts(V(G("n" + "eo"[k])), V("tn"), 1.0, A.subtract, float(CAP), A.min, off=V("nob", 2 * k, 2 * k + 1))
        ts(V("noff"), V("tn"), float(CAP + 1), A.min, off=V("nof"))
        quant(qh, 0, CAP + 2, V(ht))
        for b in PLANES[t]:
            mm(4 + b, "qe", 128 * b, qh, 0, CAP)
        for k in range(2):
            pick(G("p" + "eo"[k]), qh, V(G("n" + "eo"[k]), 0, NB // 16))
            for b in PLANES[t]:
                mm(b, "qm", 512 * k + 128 * b, G("p" + "eo"[k]), 0, NB, False, k == 1)
        for b in PLANES[t]:
            (cp if b in VCOPY[t] else act)(V("dh", DW * b + 1, DW * b + 1 + CAP), V("ps%d" % (4 + b), 0, CAP))
        new, qn = ("t2", "qy") if final else ("t1", "qb")
        runs = pairs(RUNS[t])
        for step in STEPS[t]:
            if step[0] in "qy":
                a, b = runs[step[1]]
                if step[0] == "q":
                    quant(qn, a, b, V(new, 4 * a, 4 * b))
                    mm(4 + step[1], "qv" if final else "qu", 0, qn, a, b)
                else:
                    (cp if b == C else act)(V("ysb", a, b), V("ps%d" % (4 + step[1]), 0, b - a))
                if final and b in STORES:
                    a = STORES[STORES.index(b) - 1]
                    if step[0] == "q":
                        stores.append(dma("y", T.oc[:, 4 * a:4 * b], bytes_of(V("qyc", a, b)), [V("qyc", a, b)], [], "out"))
                    else:
                        stores.append(dma("s", T.y[:, a:b], T.ysb[:, a:b], [V("ysb", a, b)], [], "out"))
                continue
            p, a, b = step[1:]
            noff, win = V("noff", a // 16, b // 16), V("dh", DW * p, DW * p + CAP + 2)
            if step[0] == "c":
                act(V(new, 4 * a + p, 4 * b, 4), V("ps%d" % p, a, b))
            elif step[0] == "g":
                act(V("gg", C * p + a, C * p + b), win, noff)
            elif step[0] == "o":
                tt(V(new, 4 * a + p, 4 * b, 4), win, V("fs", 4 * a + p, 4 * b, 4), A.add, noff)
            else:
                tt(V(new, 4 * a + p, 4 * b, 4), V("gg", C * p + a, C * p + b), V("ps%d" % p, a, b), A.add)

    for k in range(4):
        stores.append(dma("y", T.osc[4 * k:4 * k + 4, :], T.qys[32 * k:32 * k + 4, :], [V("qys")], [], "out"))
    op("y", "end", None, [], [], after=stores)
    plan(g, T, ops)
    g.wait_ge(T.sem.sent, sent[0])
